import numpy as np, ml_dtypes
CORES = [16,18,20,22]
N = 4
BF = ml_dtypes.bfloat16
def gentries(a):
    return np.ascontiguousarray(a.reshape(8, 16, -1).transpose(0, 2, 1)).reshape(8, -1)
def gtable(e):
    e = np.asarray(e); return np.ascontiguousarray(e.reshape(8, -1, 16).transpose(0, 2, 1)).reshape(128, -1).astype(np.int32)
L, S, T, H, C, X, LG = 2400, 256, 4, 4, 64, 96, 12
W = 2 ** LG; EMPTY = 16 * W - 1; OLD = 8
def parts(rng):
    z = rng.random((N, 8, 3, L)); p = 1.3 * rng.random((N, 8, 3, T * S)) - 0.15; mix = 220 * (2 * rng.random((N, 8, 16, 3)) - 1)
    w = np.clip(np.rint(128 + np.matmul(mix, z - 0.5)) + rng.integers(-6, 7, (N, 8, 16, L)), 0, 255).astype(np.int64)
    x = np.clip(np.rint(128 + np.matmul(mix, p - 0.5)) + rng.integers(-6, 7, (N, 8, 16, T * S)), 0, 255).astype(np.int64)
    ed = np.zeros((N, 8, 16, L), np.int64)
    for j in range(3):
        o = np.argsort(13 * np.floor(13 * z[:, :, j]) + np.floor(13 * z[:, :, (j + 1) % 3]) + z[:, :, (j + 2) % 3], axis=-1); at = np.argsort(o, axis=-1)
        for i in range(4): ed[:, :, 4 * j + i] = np.take_along_axis(o, (at + (1 - 2 * (i % 2)) * rng.integers(1, 7, (N, 8, L))) % L, -1)
    ids = ed[:, :, rng.permutation(12)]
    ed[:, :, :12] = np.where(rng.random(ids.shape) < 0.15, EMPTY, W * rng.integers(0, OLD + 1, ids.shape) + ids)
    ed[:, :, 12:] = (np.arange(L) + rng.integers(1, L, (N, 8, 4, L))) % L
    c = rng.integers(0, L, (N, 8, T * S, 8)); far = np.zeros(c.shape)
    for j in range(3): far = far + np.abs(np.take_along_axis(z[:, :, j], c.reshape(N, 8, -1), -1).reshape(c.shape) - p[:, :, j, :, None])
    best = np.take_along_axis(c, np.argmin(far, axis=-1)[..., None], -1)[..., 0]
    ent = np.where(rng.random(best.shape) < 0.5, best, c[..., 0])
    return w, ed, x, ent, rng.integers(100, 700, (N, 8))
def take(a, i): return np.take_along_axis(a, i[:, :, None, :], 3)
def pack(w, ed, x, ent, th):
    return {"w": np.ascontiguousarray(w.reshape(N, 128, L)).astype(np.float32).astype(BF), "nb": np.ascontiguousarray(ed.reshape(N, 128, L)).astype(np.int32),
            "x": np.ascontiguousarray(x.reshape(N, 128, T * S)).astype(np.float32).astype(BF), "ent": np.stack([gtable(a) for a in ent]),
            "th": np.repeat(th.reshape(N, 8, 1), 16, axis=2).reshape(N, 128, 1).astype(np.int32)}
def setup_inputs(rng):
    w, ed, x, ent, th = parts(rng); i = np.where(rng.random(ent.shape) < 0.15, rng.integers(0, T * S, ent.shape), np.arange(T * S))
    return pack(w, ed, take(x, i), np.take_along_axis(ent, i, -1), th)
def setup_inputs_crowd(rng):
    w, ed, x, ent, th = parts(rng); ent[..., 0] = 0; ent[..., 1] = L - 1
    pool = rng.choice(np.array([2, 5, 12, 40, 100, S, T * S]), (N, 8, 1)); pool[0, :, 0] = (1, 2, 3, 12, 40, 100, S, T * S)
    i = np.floor(rng.random(ent.shape) * pool).astype(np.int64)
    return pack(w, ed, take(x, i), np.take_along_axis(ent, i, -1), np.maximum(th - 80, 20))
def setup_inputs_room(rng):
    w, ed, x, ent, th = parts(rng); th[:] = 1; odd = np.add.reduce(w, axis=2) & 1; w[:, :, 0] = w[:, :, 0] ^ odd
    f = (0, C - 1, C, C + 1, C + X - 1, C + X, C + X + 1, S)
    for q in range(N):
        for g in range(8):
            o = rng.permutation(L); a, b = o[:S], o[S:2 * S]; n = f[g] if q == 0 else f[int(rng.integers(0, 8))]
            if n == 0 or n == S: w[q, g][:, a[-1]] = w[q, g][:, a[0]]; b[-1] = b[0]
            w[q, g][:, b] = w[q, g][:, a]; ed[q, g, 0, a] = W * rng.integers(0, OLD + 1, S) + b
            v = w[q, g][:, a]; v[3] = np.where(rng.permutation(S) < n, v[3] ^ 1, v[3])
            x[q, g, :, :S] = v; ent[q, g, :S] = a
    return pack(w, ed, x, ent, th)
def setup_inputs_ties(rng):
    w, ed, x, ent, th = parts(rng); point = rng.integers(0, 256, (N, 8, 16, 12)); point[:, :, 0] = rng.integers(0, 100, (N, 8, 12))
    w = take(point, rng.integers(0, 12, (N, 8, L))); th = rng.integers(3, 60, (N, 8))
    x = take(w, ent); x[:, :, 0] = x[:, :, 0] + th[..., None] + rng.integers(-1, 2, ent.shape)
    ent = np.where(rng.random(ent.shape) < 0.3, rng.integers(0, L, ent.shape), ent)
    h = ed[:, :, :6]; ed[:, :, 6:12] = np.where(h == EMPTY, EMPTY, W * rng.integers(0, OLD + 1, h.shape) + (h & (W - 1)))
    h = ed[:, 1::2, :12]; ed[:, 1::2, :12] = np.where(h == EMPTY, EMPTY, 4 * W + (h & (W - 1)))
    return pack(w, ed, x, ent, th)
def setup_inputs_aged(rng):
    w, ed, x, ent, th = parts(rng); x = np.tile(x[..., :S], (1, 1, 1, T)); ent = np.tile(ent[..., :S], (1, 1, T))
    th = np.where(rng.random((N, 8)) < 0.5, 4096, th)
    for q in range(N):
        for g in range(8):
            e = ed[q, g, :12]; ids = np.where(e == EMPTY, ed[q, g, 12:13], e & (W - 1)); age = rng.integers(0, OLD + 1, e.shape); i = (g + q) % 8
            if i < 3: e = np.where(e == EMPTY, EMPTY, (OLD - i) * W + ids)
            elif i == 3: e = np.full(e.shape, EMPTY)
            elif i == 4: e = age * W + ed[q, g, 12:13]
            elif i == 5: e = np.where(np.arange(12)[:, None] % 2 == 0, OLD, 0) * W + ids
            elif i == 6: e = 3 * (q % 2) * W + ids
            else: e = age * W + ids
            ed[q, g, :12] = e
    c = [int(i) for i in 1 + rng.permutation(L - 1)[:5]]; cut = [0] + c[2:]
    u = w[:, 1]; u[:, :, c + [0]] = 100; u[:, 1, c[1]] = 101
    for j in range(4): u[:, 0, cut[j]] = 140; u[:, 2 + j, cut[j]] = 160
    e = ed[:, 1]; e[:, :12, c[0]] = EMPTY; e[:, 0, c[0]] = c[1]
    for j in range(4): e[:, 12 + j, c[0]] = cut[j]
    x[:, 1] = 100; x[:, 1, 0, :S] = 180; x[:, 1, 0, S:] = 140
    for t in range(1, T): x[:, 1, 1 + t, t * S:(t + 1) * S] = 122
    ent[:, 1] = c[0]; th[:, 1] = 40
    return pack(w, ed, x, ent, th)
def setup_inputs_spread(rng):
    w, ed, x, ent, th = parts(rng)
    w = np.minimum(np.exp2(8.1 * rng.random((N, 8, 1, L))) * rng.random((N, 8, 16, L)), 255).astype(np.int64)
    x = np.minimum(np.exp2(8.1 * rng.random((N, 8, 1, T * S))) * rng.random((N, 8, 16, T * S)), 255).astype(np.int64)
    th = np.exp2(12 * rng.random((N, 8))).astype(np.int64); th[0, 0] = 0; th[1, 1] = 4096
    h = ed[:, ::2, :12]; ed[:, ::2, :12] = np.where(h == EMPTY, EMPTY, (h >> LG) * W + (np.arange(L) + rng.integers(1, L, h.shape)) % L)
    ent = np.where(rng.random(ent.shape) < 0.1, rng.choice(np.array([0, L - 1]), ent.shape), ent)
    for q in range(N):
        for g in (2, 3, 6, 7):
            w[q, g] = rng.integers(0, 4, (16, L)); x[q, g] = rng.integers(252, 256, (16, T * S))
            gone = rng.random((12, L)) < rng.choice(np.array([0.3, 0.6, 0.9, 1.0]), (1, L)); ed[q, g, :12] = np.where(gone, EMPTY, ed[q, g, :12])
            a, b = [int(c) for c in rng.permutation(L)[:2]]; i = (q + g) % 5; ent[q, g, 0] = a
            if i < 3:
                w[q, g, :, a] = 3; th[q, g] = np.add.reduce(x[q, g, :, 0]) - 48 + i - 1
            else:
                w[q, g, :, a] = 0; w[q, g, :, b] = 0; x[q, g, :, 0] = 255
                ed[q, g, :12, a] = EMPTY; ed[q, g, 12:, a] = b; th[q, g] = 4080 + i - 3
            if g >= 6: w[q, g] = 255 - w[q, g]; x[q, g] = 255 - x[q, g]
    return pack(w, ed, x, ent, th)
def check_inputs(d):
    bad = []
    for k in ("w", "x"):
        a = np.asarray(d[k]).astype(np.float32)
        if not np.all((a >= 0) & (a <= 255) & (a == np.floor(a))): bad.append("whole numbers of " + k)
    e = np.asarray(d["nb"]).astype(np.int64).reshape(N, 8, 16, L); own = np.arange(L); h = e[:, :, :12]; s = e[:, :, 12:]; c = h & (W - 1)
    if not np.all((h == EMPTY) | ((h >= 0) & (h < (OLD + 1) * W) & (c < L) & (c != own))): bad.append("edges of nb")
    if not np.all((s >= 0) & (s < L) & (s != own)): bad.append("shortcuts of nb")
    if np.min(d["ent"]) < 0 or np.max(d["ent"]) > L - 1: bad.append("range of ent")
    t = np.asarray(d["th"]).astype(np.int64).reshape(N, 8, 16)
    if np.min(t) < 0 or np.max(t) > 4096: bad.append("range of th")
    if not np.all(t == t[:, :, :1]): bad.append("th alike in a group")
    return bad
def near(wu, ed, xb, cur):
    a = np.arange(N * 8)[:, None]; c = ed[a, cur] & (W - 1)
    d = np.add.reduce(np.abs(xb[:, :, None, :] - wu[a[:, :, None], c]), axis=3)
    d = np.where(c == W - 1, 2 ** 20, d); i = np.argmin(d, axis=2)[:, :, None]
    return np.take_along_axis(c, i, 2)[:, :, 0], np.take_along_axis(d, i, 2)[:, :, 0]
def slot(e, c):
    return np.argmax(np.where((e[:, :12] & (W - 1)) == c[:, None], 16, e[:, :12] >> LG), axis=1)
def reference(w, nb, x, ent, th):
    M = N * 8; a = np.arange(M)[:, None]
    wu = np.zeros((M, W, 16), np.int32); wu[:, :L] = w.astype(np.float32).reshape(M, 16, L).transpose(0, 2, 1)
    ed = np.full((M, W, 16), EMPTY, np.int64); ed[:, :L] = nb.reshape(M, 16, L).transpose(0, 2, 1)
    xs = np.array(x.astype(np.float32).reshape(M, 16, T * S).transpose(0, 2, 1), dtype=np.int32, order="C")
    en = np.stack([gentries(b) for b in ent]).reshape(M, T * S).astype(np.int64)
    tv = th.astype(np.int64).reshape(M, 16)[:, :1]
    for t in range(T):
        xb = xs[:, t * S:(t + 1) * S]; eb = en[:, t * S:(t + 1) * S]; u = eb
        du = np.add.reduce(np.abs(xb - wu[a, u]), axis=2)
        for h in range(H):
            c, d = near(wu, ed, xb, u); go = d < du
            u = np.where(go, c, u); du = np.where(go, d, du)
        v, dv = near(wu, ed, xb, u)
        s = np.broadcast_to(np.arange(S), (M, S)); first = np.full((M, W), S)
        np.minimum.at(first, (a, u), s); np.minimum.at(first, (a, v), s)
        counts = (first[a, u] >= s) & (first[a, v] >= s)
        far = du >= tv; want = (counts & far).astype(np.int64); k = np.add.accumulate(want, axis=1) - want
        split = (want == 1) & (k < C); rest = far & ~split
        m, j = np.nonzero(counts); i = np.arange(len(m)); uu = u[m, j]; vv = v[m, j]; sp = split[m, j]; nn = L + C * t + k[m, j]
        xx = xb[m, j]; w0 = wu[m, uu]; w1 = wu[m, vv]; e0 = ed[m, uu]; e1 = ed[m, vv]; i0 = slot(e0, vv); i1 = slot(e1, uu)
        e0[:, :12] = np.where(e0[:, :12] + W >= (OLD + 1) * W, EMPTY, e0[:, :12] + W)
        e0[i, i0] = np.where(sp, nn, vv); e1[i, i1] = np.where(sp, nn, uu)
        e2 = np.full(e0.shape, EMPTY); e2[:, 0] = uu; e2[:, 1] = vv; e2[:, 12:] = e0[:, 12:]
        ed[m, uu] = e0; ed[m, vv] = e1; ed[m[sp], nn[sp]] = e2[sp]
        wu[m, uu] = w0 + ((xx - w0) >> 2); wu[m, vv] = w1 + ((xx - w1) >> 3); wu[m[sp], nn[sp]] = ((w0 + xx) >> 1)[sp]
        if t + 1 < T:
            place = np.argsort(~rest, axis=1, kind="stable")[:, :X]; num = np.add.reduce(rest.astype(np.int64), axis=1)
            kk = np.arange(X)[None, :]; q = (np.arange(N)[:, None] - 1 - kk % (N - 1)) % N
            mm = (q[:, None, :] * 8 + np.arange(8)[None, :, None]).reshape(M, X); pl = place[mm, kk]; got = num[mm] > kk
            lo, hi = (t + 2) * S - X, (t + 2) * S
            xs[:, lo:hi] = np.where(got[:, :, None], xb[mm, pl], xs[:, lo:hi]); en[:, lo:hi] = np.where(got, eb[mm, pl], en[:, lo:hi])
    P = L + T * C
    yw = np.ascontiguousarray(wu[:, :P].transpose(0, 2, 1)).reshape(N, 128, P).astype(np.float32).astype(BF)
    yn = np.ascontiguousarray(ed[:, :P].transpose(0, 2, 1)).reshape(N, 128, P).astype(np.float32)
    return {"yw": yw, "yn": yn}

@@ -1,0 +1,602 @@
+from concourse.bass import DstId, RemoteDMATransfer
+from concourse.mybir import dt, AluOpType, AxisListType, ActivationFunctionType
+
+A = AluOpType
+F = ActivationFunctionType
+T_, NB_, L_, BIG = 4, 4, 2400, 1.0e9
+FAR = 8388608.0
+MAGIC = 12582912.0
+_S = {}
+for _d, _l in (
+        ("bfloat16", "W 4096 XI0 1024 MASKB 768 IDB 128 ALB 8 BO 8 TRI 128 ONB 256 SEL 96 ZB 288 CODE 1440 WD0 8 WD1 8 WX 8 REP 2048 REP0 2048 MIX 640 CB 384 BIGI 256 "
+         "XR 3072 FARB 16 WUV 512 Z 48 W2 32 SPA 32 SPL 32 RES 16 SN 32 EXZ 768 NEQ 512 QA 512 QB 512 ZK 512 KS 512 KR 512 EQ0 256 EQ1 256 EQ2 256 EQ3 256"),
+        ("float32", "IDS 3648 PK 3648 ENTF 64 THF 1 THA 8 MASK 256 IDF 128 ALF 8 ALN 24 ALM 24 ONF 128 ADF 144 ADM 144 RST 144 RST12 384 DUM 32 DZN 16 DZR 16 "
+         "THC 1 TH128 8 BLK 128 COLS 8 KC 8 SEG 96 TA 256 TB 256 XE 256 ELX 256 NGF 512 NEGA 16 ABD 16 UVS 40 LF 32 UMD 32 EP 512 NBV 32 TG1 32 TG2 32 TG 32 "
+         "OF 192 AG 512 AH 512 KM 384 T1 256 E1 256 TGR 512 NR2 256 NA 256 AB0 256 AB1 256 AB2 256"),
+        ("int32", "NBI 2400 NBM 2400 ENT 64 THI 1 IP 256 IC 256 I16 256 IT 144 IT2 144 IJ 144 IK 96 IA 8 IB12 32 IS 16 BETA 256 GRP 256 GC 128 "
+         "N0 768 NP 768 NI 768 WNI 768 XM 288"),
+        ("uint16", "ELU 64 REPL 8 ZREP 48 K12R 32 NLST 16 LUV 32 OUV 32 ON 16 ORR 16")):
+    _l = _l.split()
+    for _i in range(0, len(_l), 2):
+        _S[_l[_i]] = (int(_l[_i + 1]), _d)
+for _c in range(2):
+    for _n, _w, _d in (("NGU", 128, "uint16"), ("GS", 512, "bfloat16"), ("DV", 1536, "bfloat16"), ("AD", 2048, "bfloat16"), ("D0", 128, "bfloat16"), ("A0", 128, "bfloat16"),
+                       ("PU", 288, "float32"), ("NR", 144, "float32"), ("EX", 128, "float32"), ("PUV", 288, "float32"),
+                       ("EXV", 128, "float32"), ("RU", 128, "float32"), ("XTN", 128, "bfloat16")):
+        _S[_n + str(_c)] = (_w, _d)
+SCRATCH, _PACK, _WIDTH = {}, {}, {"float32": 0, "bfloat16": 0, "int32": 0, "uint16": 0}
+for _n, (_w, _d) in _S.items():
+    if _n in ("XI0", "ENT", "THI"):
+        SCRATCH["D" + _n] = ("sbuf", [128, _w], _d)
+        _PACK[_n] = ("D" + _n, 0)
+    elif _w <= 768:
+        _PACK[_n] = ("A" + _d, _WIDTH[_d])
+        _WIDTH[_d] += (_w + 31) // 32 * 32
+    else:
+        SCRATCH[_n] = ("sbuf", [128, _w], _d)
+for _d, _w in _WIDTH.items():
+    SCRATCH["A" + _d] = ("sbuf", [128, _w], _d)
+for _t in range(T_ - 1):
+    SCRATCH["XC%d" % _t] = ("sbuf", [128, 352], "float32")
+    for _j in range(3):
+        SCRATCH["RX%d_%d" % (_t, _j)] = ("sbuf", [128, 96], "float32")
+_BANKS = ("K0", "K1", "S0", "S1", "L0", "L1", "M0", "M1")
+for _n in _BANKS:
+    SCRATCH[_n] = ("psum", [128, 512], "float32")
+_ENG = {"v": "sv", "s": "ss", "t": "st", "g": "sg"}
+SEMAPHORES = list(_ENG.values()) + ["dm%d" % i for i in range(12)] + ["rx%d_%d" % (t, j) for t in range(3) for j in range(3)] + ["lx%d" % t for t in range(3)]
+
+
+def rank_program(g, core, T, topo):
+    rank = T.rank_of(core)
+    if rank is None:
+        return
+    qs = {"v": g.vector, "s": g.scalar, "t": g.tensor, "g": g, "y": g.sync}
+    cnt = {}
+    known = {q: {} for q in qs}
+    hist = {}
+    unit = {}
+    acc = {}
+    for e, s in _ENG.items():
+        unit[e] = (T.sem[s], 1)
+
+    def v(name, lo=0, hi=None, st=1, p1=128, p0=0):
+        hi = hi if hi is not None else (_S[name][0] if name in _S else 512)
+        buf, off = _PACK[name] if name in _PACK else (name, 0)
+        ap = T[buf][p0:p1, lo + off:hi + off] if st == 1 else T[buf][p0:p1, lo + off:hi + off:st]
+        n = (hi - lo + st - 1) // st
+        return (ap, ((buf, off + lo, off + lo + (n - 1) * st + 1, p0, p1, st),))
+
+    def ind(w, o):
+        return (w[0].indirect(o[0]), w[1] + o[1])
+
+    def wait(q, src, i):
+        if known[q].get(src, 0) >= i:
+            return
+        sem, step = unit[src]
+        qs[q].wait_ge(sem, i * step)
+        for k, n in hist[(src, i)].items():
+            if known[q].get(k, 0) < n:
+                known[q][k] = n
+        known[q][src] = max(i, known[q].get(src, 0))
+
+    def access(q, src, outs, ins):
+        need = {}
+        for regs, wr in ((ins, False), (outs, True)):
+            for (b, lo, hi, p0, p1, st) in regs:
+                for (s2, i2, lo2, hi2, a0, a1, st2, w2) in acc.get(b, ()):
+                    if s2 == q == "t":
+                        continue
+                    if b in _BANKS and s2 != q:
+                        pass
+                    elif not (wr or w2) or lo2 >= hi or lo >= hi2 or a0 >= p1 or p0 >= a1:
+                        continue
+                    if need.get(s2, 0) < i2:
+                        need[s2] = i2
+        for s2 in sorted(need, key=lambda k: -len(hist[(k, need[k])])):
+            wait(q, s2, need[s2])
+        i = cnt.get(src, 0) + 1
+        cnt[src] = i
+        hist[(src, i)] = dict(known[q])
+        for regs, wr in ((ins, False), (outs, True)):
+            for (b, lo, hi, p0, p1, st) in regs:
+                keep = []
+                for r in acc.get(b, ()):
+                    if wr and st == 1 and lo <= r[2] and r[3] <= hi and p0 <= r[4] and r[5] <= p1:
+                        continue
+                    if r[0] == src and r[7] == wr and r[2:6] == (lo, hi, p0, p1):
+                        continue
+                    keep.append(r)
+                keep.append((src, i, lo, hi, p0, p1, st, wr))
+                acc[b] = keep
+
+    def emit(q, outs, ins, call):
+        access(q, q, outs, ins)
+        call().then_inc(unit[q][0], 1)
+
+    nd = [0]
+
+    def dma(q, out, in_, outs, ins):
+        src = "d%d" % nd[0]
+        unit[src] = (T.sem["dm%d" % nd[0]], 16)
+        nd[0] += 1
+        access(q, src, outs, ins)
+        qs[q].dma_start(out=out, in_=in_).then_inc(unit[src][0], 16)
+
+    def tt(o, a, b, op):
+        emit("v", o[1], a[1] + b[1], lambda: g.vector.tensor_tensor(out=o[0], in0=a[0], in1=b[0], op=op))
+
+    def ts(o, a, s1, op0, s2=None, op1=None):
+        ins, x1 = a[1], s1
+        if isinstance(s1, tuple):
+            ins, x1 = ins + s1[1], s1[0]
+        if op1 is None:
+            emit("v", o[1], ins, lambda: g.vector.tensor_scalar(out=o[0], in0=a[0], scalar1=x1, scalar2=None, op0=op0))
+        else:
+            emit("v", o[1], ins, lambda: g.vector.tensor_scalar(out=o[0], in0=a[0], scalar1=x1, scalar2=s2, op0=op0, op1=op1))
+
+    def tc(o, a):
+        emit("v", o[1], a[1], lambda: g.vector.tensor_copy(out=o[0], in_=a[0]))
+
+    def scat(w, o, a, flag=False):
+        if flag:
+            emit("v", w[1], o[1] + a[1], lambda: g.vector.tensor_scalar(out=w[0].indirect(o[0]), in0=a[0], scalar1=1.0, scalar2=1048576.0, op0=A.mult, op1=A.add))
+        else:
+            emit("v", w[1], o[1] + a[1], lambda: g.vector.tensor_copy(out=w[0].indirect(o[0]), in_=a[0]))
+
+    def scan(o, d0, d1, init, op0, op1):
+        emit("v", o[1], d0[1] + d1[1], lambda: g.vector.tensor_tensor_scan(out=o[0], data0=d0[0], data1=d1[0], initial=init, op0=op0, op1=op1))
+
+    def fill(o, x):
+        emit("v", o[1], (), lambda: g.vector.memset(o[0], x))
+
+    def act(o, a, f=F.Copy, bias=None, scale=None):
+        ins, kw = a[1], {}
+        for k, x in (("bias", bias), ("scale", scale)):
+            if isinstance(x, tuple):
+                ins, kw[k] = ins + x[1], x[0]
+            elif x is not None:
+                kw[k] = x
+        emit("s", o[1], ins, lambda: g.scalar.activation(out=o[0], in_=a[0], func=f, **kw))
+
+    def mm(o, l, r, start=True, stop=True):
+        emit("t", o[1], l[1] + r[1], lambda: g.tensor.matmul(out=o[0], lhsT=l[0], rhs=r[0], start=start, stop=stop))
+
+    def one(name, lo, hi):
+        return v(name, lo, hi, 1, 1)
+
+    def close(name, lo, hi):
+        mm(v(name, lo, hi), one("ONB", 0, 128), one("ZB", 0, hi - lo), False, True)
+
+    def iota(o, pat, base, cm):
+        emit("g", o[1], (), lambda: g.iota(o[0], pat, base, cm))
+
+    dma("s", T.DXI0[:, :], T.x[:, :], v("XI0")[1], ())
+    dma("s", T.DENT[:, :], T.ent[:, :], v("ENT")[1], ())
+    for to, frm, name in ((T.NBI, T.nb, "NBI"), (T.W, T.w, "W")):
+        for lo, hi, q in ((0, 1200, "y"), (1200, 2400, "s")):
+            dma(q, to[:, lo:hi], frm[:, lo:hi], v(name, lo, hi)[1], ())
+    dma("y", T.DTHI[:, :], T.th[:, :], v("THI")[1], ())
+
+    fill(v("REP0"), 1.0)
+    fill(v("ONB"), 1.0)
+    iota(v("IP"), [[0, 256]], 0, 1)
+    iota(v("IC"), [[1, 256]], 0, 0)
+    emit("g", v("REP")[1], v("REP0")[1], lambda: g.affine_select(v("REP")[0], v("REP0")[0], [[1, 128], [0, 16]], A.is_equal, 0.0, 0, -1))
+    iota(v("I16"), [[0, 16], [1, 16]], 0, 0)
+    iota(v("IT"), [[16, 8], [1, 18]], -2, 0)
+    iota(v("IJ"), [[0, 8], [1, 18]], 0, 0)
+    iota(v("IA"), [[18, 8]], 17, 0)
+    iota(v("IS"), [[16, 16]], 0, 0)
+    iota(v("IK"), [[16, 8], [1, 12]], 0, 0)
+    iota(v("IB12"), [[12, 32]], 11, 0)
+    tt(v("IDB"), v("IP", 0, 128), v("IC", 0, 128), A.is_equal)
+    ts(v("GRP"), v("IP"), 4, A.arith_shift_right)
+    tt(v("ALF"), v("GRP", 0, 8), v("IC", 0, 8), A.is_equal)
+    ts(v("BETA"), v("IP"), 15, A.bitwise_and)
+    ts(v("BO"), v("ALF"), 128.0, A.mult)
+    tc(v("ZREP"), v("IC", 0, 48))
+    tc(v("IDF"), v("IDB"))
+    fill(v("CODE"), 0.0)
+    fill(v("ZB"), 0.0)
+    fill(v("RST"), 0.0)
+    fill(v("RST", 0, 144, 18), BIG)
+    fill(v("W", 2400, 4096), 0.0)
+    fill(v("W", 4088, 4096), 1024.0)
+    fill(v("IDS", 2400, 2656), 0.0)
+    tc(v("ELU"), v("ENT"))
+    tc(v("ENTF"), v("ENT"))
+
+    def prep_x(t, c, blocks):
+        xtn = v("XTN%d" % c)
+        if 0 in blocks or c == 1:
+            mm(v("M1", 256, 384), v("XI0", 256 * t + 128 * c, 256 * t + 128 * c + 128), v("IDB"))
+            act(xtn, v("M1", 256, 384), F.Identity, scale=-1.0)
+        for b in blocks:
+            bank, sb, lo = v("M%d" % (b % 2)), (0, 1, 3)[b], 1536 * c + 512 * b
+            mm(bank, xtn, v("REP", 512 * sb, 512 * sb + 512))
+            act(v("XR", lo, lo + 512), bank, F.Identity, scale=-1.0)
+
+    def prep_l(t):
+        tt(v("ELX"), ind(v("ENTF", 16 * t, 16 * t + 16), v("ZREP", 0, 16)), v("MASK"), A.mult)
+
+    def prep_e(t, lo):
+        mm(v("M1", lo, 256), v("BLK"), v("ELX", lo, 256), True, False)
+        mm(v("M1", lo, 256), v("IDB"), v("XI0", 256 * t + lo, 256 * t + 256), False, True)
+        act(v("XE", lo, 256), v("M1", lo, 256))
+
+    prep_x(0, 0, (0, 1, 2))
+    prep_x(0, 1, (0, 1, 2))
+    tt(v("MASK"), v("BETA"), v("I16"), A.is_equal)
+    tc(v("REPL"), v("IA"))
+    for e in range(5):
+        b = 288 * e
+        ts(v("CODE", b, b + 144), v("IJ"), float(16 * e if e < 4 else 0), A.add)
+        fill(v("CODE", b, b + 144, 18), 0.0 if e < 4 else FAR)
+        fill(v("CODE", b + 17, b + 144, 18), FAR)
+    ts(v("IT2"), v("IT"), 1.0, A.add)
+    tt(v("ADF"), v("IP", 0, 144), v("IT"), A.is_equal)
+    tt(v("ADM"), v("IP", 0, 144), v("IT2"), A.is_equal)
+    for n, j in (("ADF", 0), ("ADF", 1), ("ADM", 0), ("ADM", 17)):
+        fill(v(n, j, 144, 18), 0.0)
+    tt(v("ADF"), v("ADF"), v("ADM"), A.subtract)
+    ts(v("GC"), v("IC", 0, 128), 4, A.arith_shift_right)
+    tt(v("BLK"), v("GRP", 0, 128), v("GC"), A.is_equal)
+    ts(v("BLK"), v("BLK"), 256.0, A.mult)
+    prep_l(0)
+    prep_e(0, 0)
+    for lo in (0, 1200):
+        ts(v("NBM", lo, lo + 1200), v("NBI", lo, lo + 1200), 4095, A.bitwise_and)
+        tc(v("IDS", lo, lo + 1200), v("NBM", lo, lo + 1200))
+
+    def late_constants():
+        fill(v("PK", 2400, 2656), 65535.0)
+        for lo in (0, 1200):
+            tc(v("PK", lo, lo + 1200), v("NBI", lo, lo + 1200))
+        tc(v("ALB"), v("ALF"))
+        for n, k in (("ALN", (1.0, -1.0, -1.0)), ("ALM", (0.0, -1.0, 1.0))):
+            for i, x in enumerate(k):
+                ts(v(n, 8 * i, 8 * i + 8), v("ALF"), x, A.mult)
+        tt(v("TRI"), v("IP", 0, 128), v("IC", 0, 128), A.is_le)
+        for i in range(3):
+            tc(v("MASKB", 256 * i, 256 * i + 256), v("MASK"))
+        for i, x in enumerate((262144.0, -262144.0)):
+            ts(v("BIGI", 128 * i, 128 * i + 128), v("IDB"), x, A.mult)
+        tt(v("SEL"), v("IP", 0, 96), v("IK"), A.is_equal)
+        fill(v("RST12"), 0.0)
+        fill(v("RST12", 0, 384, 12), BIG)
+        tc(v("K12R"), v("IB12"))
+        for i, k in ((0, 16.0), (1, 0.0)):
+            ts(v("TA", 16 * i, 16 * i + 16), v("IC", 0, 16), k - 32.0, A.add)
+            ts(v("TB", 16 * i, 16 * i + 16), v("BETA", 0, 16), float(i), A.is_equal)
+        tt(v("TA", 0, 32), v("TA", 0, 32), v("TB", 0, 32), A.mult)
+        tt(v("TB", 32, 48), v("TA", 0, 16), v("TA", 16, 32), A.add)
+        ts(v("NLST"), v("TB", 32, 48), 32.0, A.add)
+        fill(v("UVS", 32, 40), 0.0)
+        tt(v("TA", 64, 80), v("IS"), v("BETA", 0, 16), A.add)
+        for n, lo, x in (("DUM", 0, 2656.0), ("DUM", 16, 2912.0), ("DZN", 0, 801.0), ("DZR", 0, 97.0)):
+            ts(v(n, lo, lo + 16), v("TA", 64, 80), x, A.add)
+        for per, top in ((16, 2.0 ** 62), (32, 0.8 * 2.0 ** 64)):
+            fill(v("TA", 0, 128), 0.25)
+            fill(v("TA", 0, 128, per), 0.0)
+            fill(v("TB", 0, 128), 0.0)
+            fill(v("TB", 0, 128, per), top)
+            scan(v("TA", 128, 256), v("TA", 0, 128), v("TB", 0, 128), 0.0, A.mult, A.add)
+            tt(v("TB", 128, 256), v("TA", 128, 256), v("IDF"), A.mult)
+            if per == 16:
+                mm(v("M1", 0, 8), v("TB", 128, 256), v("ALF"))
+                tc(v("WD0"), v("M1", 0, 8))
+                ts(v("WD1"), v("WD0"), 2.0 ** -32, A.mult)
+                ts(v("WX"), v("ALF"), 2.0 ** 64, A.mult)
+            else:
+                o, a = v("THC"), v("TB", 128, 256)
+                emit("v", o[1], a[1], lambda: g.vector.tensor_reduce(out=o[0], in_=a[0], axis=AxisListType.X, op=A.add))
+        for i, x in enumerate((0.75, 0.25, 0.875, 0.125, 0.5)):
+            ts(v("MIX", 128 * i, 128 * i + 128), v("IDB"), x, A.mult)
+        for i, x in enumerate((-3.0 / 1024, -7.0 / 2048, -1.0 / 512)):
+            fill(v("CB", 128 * i, 128 * i + 128), x)
+        b1 = v("BETA", 0, 1)
+        ts(v("COLS", 3, 4), b1, 12.0, A.is_ge)
+        ts(v("COLS", 5, 6), v("COLS", 3, 4), 512.0, A.mult)
+        tt(v("COLS", 0, 1), v("COLS", 5, 6), b1, A.add)
+        ts(v("COLS", 1, 2), v("COLS", 3, 4), -1.0e20, A.mult, -2147418112.0, A.add)
+        ts(v("COLS", 2, 3), v("COLS", 3, 4), -4096.0, A.mult, 4096.0, A.add)
+        ts(v("COLS", 6, 7), b1, 2.0, A.is_ge)
+        tt(v("COLS", 7, 8), v("COLS", 6, 7), v("COLS", 3, 4), A.subtract)
+        ts(v("COLS", 4, 5), v("COLS", 7, 8), 65535.0, A.mult)
+        for i, x in enumerate((-2047.5 / 4096, MAGIC, 16 * (MAGIC + 9), 16.0, -131072.0)):
+            fill(v("KC", i, i + 1), x)
+        fill(v("SEG"), 1.0)
+        fill(v("SEG", 0, 96, 16), 0.0)
+        for t in range(T_ - 1):
+            fill(v("XC%d" % t, 0, 96), -1.0)
+        fill(v("ONF"), 1.0)
+        tc(v("THF"), v("THI"))
+        ts(v("THA"), v("ALF"), v("THF"), A.mult, 8.0, A.mult)
+        mm(v("M1", 16, 24), v("ONF"), v("THA"))
+        tc(v("TH128"), v("M1", 16, 24))
+
+    w_win, id_win, pk_win = v("W"), v("IDS", 0, 2656), v("PK", 0, 2656)
+
+    def gather_sub(c, b):
+        sb = (0, 1, 3)[b]
+        tt(v("DV%d" % c, 512 * b, 512 * b + 512), ind(w_win, v("NGU%d" % c, 32 * sb, 32 * sb + 32)),
+           v("XR", 1536 * c + 512 * b, 1536 * c + 512 * b + 512), A.subtract)
+
+    def absd(c, sb):
+        src = v("S%d" % c) if sb == 2 else v("DV%d" % c, 512 * min(sb, 2), 512 * min(sb, 2) + 512)
+        act(v("AD%d" % c, 512 * sb, 512 * sb + 512), src, F.Abs)
+
+    def dist(c, b0, b1):
+        for i in range(16):
+            mm(v("K%d" % c, 1 + i, 144, 18, 32 * b1, 32 * b0), v("AD%d" % c, 512 * b0 + i, 512 * b1, 16), v("BO"), False, False)
+
+    def front1(t, e, c):
+        k = "K%d" % c
+        ul = v("ELU", 16 * t + 8 * c, 16 * t + 8 * c + 8) if e == 0 else v("LUV", 8 * c, 8 * c + 8)
+        ngf = v("NGF", 128 * c, 128 * c + 128)
+        tc(v("NGU%d" % c), ind(id_win, ul))
+        act(ngf, ind(id_win, ul))
+        act(v("GS%d" % c), ind(w_win, v("NGU%d" % c, 64, 96)))
+        gather_sub(c, 0)
+        mm(v(k, 0, 287), one("ONB", 0, 128), one("CODE", 288 * e, 288 * e + 287), True, False)
+        if e == 0:
+            mm(v(k, 144, 287, 18), v("ELX", 128 * c, 128 * c + 128), v("ALF"), False, False)
+        elif e < 4:
+            mm(v(k, 0, 287, 18), v("IDF"), v("PU%d" % c, 17, 288, 18), False, False)
+        absd(c, 0)
+        mm(v("S%d" % c), v("XTN%d" % c), v("REP", 1024, 1536), True, False)
+        mm(v("S%d" % c), v("IDB"), v("GS%d" % c), False, True)
+        mm(v(k, 143, 287), ngf, v("ADF"), False, False)
+        gather_sub(c, 1)
+        if e == 0:
+            tt(v("D0%d" % c), ind(w_win, ul), v("XI0", 256 * t + 128 * c, 256 * t + 128 * c + 128), A.subtract)
+        absd(c, 1)
+        absd(c, 2)
+        if e == 0:
+            act(v("A0%d" % c), v("D0%d" % c), F.Abs)
+            mm(v(k, 0, 144, 18), v("A0%d" % c), v("BO"), False, False)
+
+    def front2(c):
+        dist(c, 0, 3)
+        gather_sub(c, 2)
+        absd(c, 3)
+        dist(c, 3, 4)
+        close("K%d" % c, 0, 287)
+
+    def post1(e, c):
+        k = "K%d" % c
+        pu, x = ("PU%d" % c, v("EX%d" % c)) if e < 4 else ("PUV%d" % c, v("EXV%d" % c))
+        p, u, nr = v(pu, 0, 144), v(pu, 144, 288), v("NR%d" % c)
+        scan(p, v("RST"), v(k, 0, 144), BIG, A.max, A.min)
+        tt(nr, p, v(k, 0, 144), A.is_lt)
+        scan(u, v(k, 143, 287), nr, 0.0, A.add, A.mult)
+        tt(x, ind(u, v("REPL")), v("MASK", 0, 128), A.mult)
+        if e < 4:
+            mm(v("L%d" % c, 0, 8), x, v("ALF"))
+        else:
+            mm(v("L%d" % c, 0, 24), x, v("ALN"), True, False)
+            mm(v("L%d" % c, 0, 24), v("EX%d" % c), v("ALM"), False, True)
+
+    def rows(c, pu, x):
+        act(v("RU%d" % c), ind(v(pu, 144, 288), v("REPL")))
+        mm(v("M%d" % c, x, 256, 2), v("RU%d" % c), v("IDF"))
+
+    def post2(e, c):
+        if e < 4:
+            tc(v("LUV", 8 * c, 8 * c + 8), v("L%d" % c, 0, 8))
+        else:
+            rows(c, "PUV%d" % c, 1)
+            act(v("NEGA", 8 * c, 8 * c + 8), v("L%d" % c, 8, 16))
+            act(v("ABD", 8 * c, 8 * c + 8), v("L%d" % c, 16, 24), F.Abs)
+            tc(v("LUV", 16 + 8 * c, 24 + 8 * c), v("L%d" % c, 0, 8))
+
+    def winners(c):
+        tt(v("FARB", 8 * c, 8 * c + 8), v("PU%d" % c, 17, 144, 18), v("TH128"), A.is_ge)
+        rows(c, "PU%d" % c, 0)
+        act(v("UVS", 16 + 8 * c, 24 + 8 * c), v("PU%d" % c, 161, 288, 18))
+        act(v("EP", 128 * c, 128 * c + 128), ind(pk_win, v("LUV", 8 * c, 8 * c + 8)))
+
+    def put(name, t, src):
+        base = L_ + 64 * t
+        scat(v(name, 0, 3168), v("OUV"), v(src, 0, 512))
+        scat(v(name, base, base + 1056), v("ON"), v(src, 512, 768))
+
+    def merge(t):
+        for j in range(3):
+            tt(v("XM", j, 96, 3), v("RX%d_%d" % (t - 1, j), j, 96, 3), v("XE", 160 + j, 256, 3), A.max)
+        ts(v("XM", 96, 192), v("XM", 0, 96), 255, A.bitwise_and)
+        ts(v("XM", 192, 288), v("XM", 0, 96), 8, A.logical_shift_right, 4095, A.bitwise_and)
+        tc(v("XI0", 256 * t + 160, 256 * t + 256), v("XM", 96, 192))
+        tt(v("ELX", 160, 256), v("XM", 192, 288), v("MASK", 160, 256), A.mult)
+        scan(v("OF", 0, 96), v("SEG"), v("ELX", 160, 256), 0.0, A.mult, A.add)
+        tc(v("ELU", 16 * t + 10, 16 * t + 16), v("OF", 15, 96, 16))
+        prep_x(t, 1, (1, 2))
+        prep_e(t, 160)
+
+    def walks(t):
+        prev = None
+        for e in range(5):
+            for c in range(2):
+                if t and e == 0 and c == 1:
+                    put("PK", t - 1, "NP")
+                    merge(t)
+                front1(t, e, c)
+                if prev:
+                    post1(*prev)
+                front2(c)
+                if prev:
+                    post2(*prev)
+                if t == 0 and e == 0 and c == 1:
+                    late_constants()
+                if e == 4:
+                    winners(c)
+                prev = (e, c)
+        post1(*prev)
+        count(range(4), 0)
+        post2(*prev)
+        count(range(4, 8), 0)
+        count(range(8), 1)
+        count(range(8, 16), 1)
+
+    nc = [0]
+
+    def count(blocks, rc):
+        if blocks[0] == 0 and rc == 0:
+            mm(v("K0", 480, 496), one("ONB", 0, 128), one("ZB", 0, 16), True, False)
+        for a in blocks:
+            own = a // 8 == rc
+            lo = 64 * (a // 2 % 4) if own else 0
+            ab, eq, r = v("AB%d" % (nc[0] % 3), 0, 256 - lo), "EQ%d" % (nc[0] % 4), lo // 2
+            nc[0] += 1
+            act(ab, v("M%d" % rc, lo, 256), F.Abs, bias=v("NEGA", a, a + 1), scale=2.0)
+            ts(v(eq, 0, 256 - lo), ab, v("ABD", a, a + 1), A.is_equal)
+            part = [(0, 128, "WX")]
+            if own:
+                part = [(r, 32, "WD%d" % (a % 2))]
+                part += [(r2, n2, "WX") for r2, n2 in {0: ((32, 32), (64, 64)), 32: ((64, 64),), 64: ((96, 32),), 96: ()}[r]]
+            for pr, pn, wt in part:
+                s0 = 2 * pr - lo
+                for x in range(2):
+                    mm(v("K0", 480 + 8 * rc, 488 + 8 * rc, 1, pr + pn, pr), v(eq, s0 + x, s0 + 2 * pn, 2), v(wt), False, False)
+        if blocks[-1] == 15:
+            close("K0", 480, 496)
+
+    def offsets(lo, dz, out):
+        z, o, o2 = v("L0", lo, lo + 16), v("OF", lo, lo + 16), v("OF", lo + 64, lo + 80)
+        ts(o, z, 0.0, A.is_equal)
+        tt(o2, o, dz, A.mult)
+        tt(o, o2, z, A.add)
+        ts(out, o, -1.0, A.add)
+
+    def lists(kind, lo):
+        for c in range(2):
+            j = 128 * (2 * kind + c)
+            mm(v("L0", lo + 8 * c, lo + 8 * c + 8), v("EXZ", j, j + 128), v("ALB"))
+
+    def send(t):
+        tr, src, n = [], v("XC%d" % t, 0, 96), 4
+        for j in range(3):
+            dst = T.cores[(rank + 1 + j) % NB_]
+            rid, pid = topo.addr(dst)[:2]
+            eng = topo.engines(core, dst)
+            n = 4 if len(eng) >= 12 else 2
+            m = sum(1 << x for x in eng[n * j:n * j + n])
+            key, b = "r%d_%d" % (t, j), "RX%d_%d" % (t, j)
+            unit[key] = (T.sem["rx%d_%d" % (t, j)], n)
+            hist[(key, 1)] = {}
+            cnt[key] = 1
+            acc[b] = [(key, 1, 0, 96, 0, 128, 1, True)]
+            tr.append(RemoteDMATransfer(dst_ids=[DstId(rid=rid, pnc=pid)], dma_engine_mask=m, remote_sem=T.sem["rx%d_%d" % (t, j)], src=src[0], dst=T[b][:, 0:96]))
+        unit["l%d" % t] = (T.sem["lx%d" % t], 3 * n)
+        access("g", "l%d" % t, (), src[1])
+        g.remote_dma_fused(tr, local_sem=T.sem["lx%d" % t])
+
+    def edit(t):
+        last, base = t == T_ - 1, L_ + 64 * t
+        vl = v("LUV", 16, 32)
+        act(v("EP", 256, 512), ind(pk_win, vl))
+        act(v("NGF", 256, 512), ind(id_win, vl))
+        act(v("AG"), v("EP"), F.Identity, bias=v("KC", 0, 1), scale=1.0 / 4096)
+        act(v("AH"), v("AG"), F.Identity, bias=v("KC", 1, 2))
+        act(v("QA"), v("AH"), F.Relu, bias=v("KC", 2, 3), scale=-16.0)
+        act(v("QB"), v("QA"), F.Identity, bias=v("KC", 3, 4))
+        for c in range(2):
+            act(v("UVS", 8 * c, 8 * c + 8), v("PUV%d" % c, 161, 288, 18))
+        act(v("WUV"), ind(w_win, v("LUV")))
+        ts(v("Z", 0, 16), v("K0", 480, 496), v("THC"), A.is_lt)
+        for i in range(2):
+            tt(v("W2", 16 * i, 16 * i + 16), v("Z", 0, 16), v("FARB"), A.mult)
+        mm(v("L1", 0, 32), v("TRI"), v("W2"), True, False)
+        mm(v("L1", 8, 16), v("ONB", 0, 128), v("W2", 0, 8), False, False)
+        mm(v("L1", 24, 32), v("ONB", 0, 128), v("W2", 16, 24), False, False)
+        close("L1", 0, 32)
+        tc(v("LF"), v("LUV"))
+        tt(v("UMD"), v("LF"), v("DUM"), A.subtract)
+        ts(v("SPA"), v("L1", 0, 32), 64.0, A.is_le)
+        tt(v("SPL"), v("SPA"), v("W2"), A.mult)
+        tt(v("Z", 16, 32), v("SPL", 0, 16), v("L1", 0, 16), A.mult)
+        ts(v("NBV"), v("L1", 0, 32), float(base - 1), A.add)
+        if not last:
+            tt(v("RES"), v("FARB"), v("SPL", 0, 16), A.subtract)
+            mm(v("L1", 64, 80), v("TRI"), v("RES"), True, False)
+            mm(v("L1", 72, 80), v("ONB", 0, 128), v("RES", 0, 8), False, False)
+            close("L1", 64, 80)
+        for c in range(2):
+            for y in range(2):
+                j = 256 * y + 128 * c
+                tt(v("NEQ", j, j + 128), v("NGF", j, j + 128), v("M%d" % c, 1 - y, 256, 2), A.not_equal)
+        if not last:
+            ts(v("SN", 0, 16), v("L1", 64, 80), 96.0, A.is_le)
+            tt(v("SN", 16, 32), v("SN", 0, 16), v("RES"), A.mult)
+            tt(v("Z", 32, 48), v("SN", 16, 32), v("L1", 64, 80), A.mult)
+            tt(v("EXZ", 512, 768), ind(v("Z", 32, 48), v("ZREP", 0, 16)), v("MASKB", 512, 768), A.mult)
+            lists(2, 48)
+        tt(v("EXZ", 0, 512), ind(v("Z", 0, 32), v("ZREP", 0, 32)), v("MASKB", 0, 512), A.mult)
+        if not last:
+            offsets(48, v("DZR"), v("ORR"))
+            scat(v("XC%d" % t, 0, 352), v("ORR"), v("XE"), True)
+            send(t)
+        lists(0, 0)
+        lists(0, 16)
+        lists(1, 32)
+        tt(v("ZK"), v("NEQ"), v("QB"), A.mult)
+        act(v("KS"), v("ZK"), F.Identity, bias=v("COLS", 0, 1))
+        for b in range(4):
+            mm(v("K0", 96 * b, 96 * b + 96), v("KS", 128 * b, 128 * b + 128), v("SEL"))
+        tt(v("TG1"), v("NBV"), v("UVS", 0, 32), A.subtract)
+        tt(v("TG2"), v("SPL"), v("TG1"), A.mult)
+        tt(v("TG"), v("TG2"), v("UVS", 0, 32), A.add)
+        act(v("TGR"), ind(v("TG"), v("ZREP", 0, 32)), F.Identity, bias=v("KC", 4, 5))
+        xs = v("XI0", 256 * t, 256 * t + 256)
+        for bank, lo, a, f1, f2, k in (("S1", 0, 0, 0, 1, 0), ("S1", 256, 256, 2, 3, 1), ("S0", 0, 0, 4, 4, 2)):
+            o = v(bank, lo, lo + 256)
+            mm(o, v("MIX", 128 * f1, 128 * f1 + 128), v("WUV", a, a + 256), True, False)
+            mm(o, v("MIX", 128 * f2, 128 * f2 + 128), xs, False, False)
+            mm(o, v("CB", 128 * k, 128 * k + 128), v("ONB"), False, True)
+        scan(v("KM"), v("RST12"), v("K0", 0, 384), BIG, A.max, A.min)
+        act(v("KR"), ind(v("KM"), v("K12R")))
+        for b in range(4):
+            k1, j = v("K1", 128 * b, 128 * b + 128), 128 * b
+            mm(k1, v("BIGI", 0, 128), v("KS", j, j + 128), True, False)
+            mm(k1, v("KR", j, j + 128), v("BIGI", 128, 256), False, False)
+            mm(k1, v("TGR", j, j + 128), v("IDF"), False, True)
+        tt(v("OF", 128, 160), v("L0", 0, 32), v("UMD"), A.mult)
+        tt(v("OF", 160, 192), v("OF", 128, 160), v("DUM"), A.add)
+        tc(v("OUV"), v("OF", 160, 192))
+        offsets(32, v("DZN"), v("ON"))
+        tc(v("WNI", 0, 512), v("S1"))
+        tc(v("WNI", 512, 768), v("S0", 0, 256))
+        act(v("T1"), v("EP", 0, 256), F.Relu, bias=v("COLS", 1, 2), scale=65536.0)
+        act(v("NA"), v("EP", 0, 256), F.Identity, bias=v("COLS", 4, 5), scale=v("COLS", 3, 4))
+        for c in range(2):
+            nr2 = v("NR2", 128 * c, 128 * c + 128)
+            act(nr2, ind(v("UVS"), v("NLST", 8 * c, 8 * c + 8)))
+            mm(v("L1", 256 + 128 * c, 384 + 128 * c), nr2, v("IDF"))
+        if not last:
+            prep_l(t + 1)
+            prep_x(t + 1, 0, (0, 1, 2))
+            prep_e(t + 1, 0)
+            prep_x(t + 1, 1, (0,))
+        put("W", t, "WNI")
+        if last:
+            for lo, hi, q in ((0, 1328, "y"), (1328, 2656, "s")):
+                dma(q, T.yw[:, lo:hi], T.W[:, lo:hi], (), v("W", lo, hi)[1])
+        tt(v("E1"), v("EP", 0, 256), v("T1"), A.add)
+        ts(v("EP", 0, 256), v("E1"), v("COLS", 2, 3), A.add, 65535.0, A.min)
+        tt(v("N0", 512, 768), v("NA"), v("L1", 256, 512), A.add)
+        tt(v("N0", 0, 512), v("EP"), v("K1"), A.min)
+        if not last:
+            ts(v("NI"), v("N0"), 4095, A.bitwise_and)
+            put("IDS", t, "NI")
+        ts(v("NP"), v("N0"), 131071, A.bitwise_and)
+        if last:
+            put("PK", t, "NP")
+            for lo, hi, q in ((0, 1328, "y"), (1328, 2656, "s")):
+                dma(q, T.yn[:, lo:hi], T.PK[:, lo:hi], (), v("PK", lo, hi)[1])
+
+    for t in range(T_):
+        walks(t)
+        edit(t)
+    for src in sorted(cnt):
+        wait("g", src, cnt[src])

@@ -8,14 +8,14 @@ FAR = 8388608.0
 MAGIC = 12582912.0
 _S = {}
 for _d, _l in (
-        ("bfloat16", "W 4096 XI0 1024 MASKB 768 IDB 128 ALB 8 BO 8 TRI 128 ONB 256 SEL 96 ZB 288 CODE 1440 WD0 8 WD1 8 WX 8 REP 2048 REP0 2048 MIX 640 CB 384 BIGI 256 "
-         "XR 3072 FARB 16 WUV 512 Z 48 W2 32 SPA 32 SPL 32 RES 16 SN 32 EXZ 768 NEQ 512 QA 512 QB 512 ZK 512 KS 512 KR 512 EQ0 256 EQ1 256 EQ2 256 EQ3 256"),
-        ("float32", "IDS 3648 PK 3648 ENTF 64 THF 1 THA 8 MASK 256 IDF 128 ALF 8 ALN 24 ALM 24 ONF 128 ADF 144 ADM 144 RST 144 RST12 384 DUM 32 DZN 16 DZR 16 "
-         "THC 1 TH128 8 BLK 128 COLS 8 KC 8 SEG 96 TA 256 TB 256 XE 256 ELX 256 NGF 512 NEGA 16 ABD 16 UVS 40 LF 32 UMD 32 EP 512 NBV 32 TG1 32 TG2 32 TG 32 "
-         "OF 192 AG 512 AH 512 KM 384 T1 256 E1 256 TGR 512 NR2 256 NA 256 AB0 256 AB1 256 AB2 256"),
-        ("int32", "NBI 2400 NBM 2400 ENT 64 THI 1 IP 256 IC 256 I16 256 IT 144 IT2 144 IJ 144 IK 96 IA 8 IB12 32 IS 16 BETA 256 GRP 256 GC 128 "
-         "N0 768 NP 768 NI 768 WNI 768 XM 288"),
-        ("uint16", "ELU 64 REPL 8 ZREP 48 K12R 32 NLST 16 LUV 32 OUV 32 ON 16 ORR 16")):
+        ("bfloat16", "W 4096 XI0 1024 MASKB 256 IDB 128 ALB 8 BO 8 TRI 128 ONB 256 SEL 96 ZB 288 CODE 1440 WD0 8 WD1 8 WX 8 REP 2048 MIX 640 CB 384 BIGI 256 "
+         "XR 3072 FARB 16 WUV 512 Z 48 W2 32 SPA 32 SPL 32 RES 16 SN 32 EXZ 512 EQ0 256 EQ1 256 EQ2 256 EQ3 256 "
+         "AGE 512 ZK 512 KR 512 I16 256 J8 8 KX 64 CR2 128 RC2 96 C0 512 C1 512 WNB 512"),
+        ("float32", "IDS 3168 PK 3168 ENTF 64 THF 1 THA 8 MASK 256 IDF 128 ALF 8 ALN 24 ALM 24 ONF 128 ADF 144 ADM 144 RST 144 RST12 384 DUM 32 DZR 16 "
+         "THC 1 TH128 8 BLK 128 COLS 8 KC 8 SEG 96 TA 256 TB 256 XE 256 ELX 1024 NGF 512 NEGA 16 ABD 16 UVS 40 LF 32 UMD 32 EP 512 EPU 256 NBV 32 TG1 32 TG2 32 TG 32 "
+         "OF 192 KM 384 T1 256 AQ 256 TGR 512 NR2 256 NA 256 NX 288 HX 288 R1 768 PC 16 AB0 256 AB1 256 AB2 256 GRPF 1 BETF 1 BI0 1 BI1 1"),
+        ("int32", "NBI 2400 NBM 2400 ENT 64 THI 1 IP1 1 GRP1 1 BET1 1 IC 48 IA 8 IB12 32 IS 16 N0 512 NI 512 XM 288 QI 64"),
+        ("uint16", "ELU 64 REPL 8 ZREP 48 K12R 32 NLST 16 LUV 32 OUV 32 ORR 16 NL 4")):
     _l = _l.split()
     for _i in range(0, len(_l), 2):
         _S[_l[_i]] = (int(_l[_i + 1]), _d)
@@ -165,11 +165,20 @@ def rank_program(g, core, T, topo):
     def one(name, lo, hi):
         return v(name, lo, hi, 1, 1)
 
+    def two(name, lo, hi):
+        return v(name, lo, hi, 1, 2)
+
     def close(name, lo, hi):
         mm(v(name, lo, hi), one("ONB", 0, 128), one("ZB", 0, hi - lo), False, True)
 
     def iota(o, pat, base, cm):
         emit("g", o[1], (), lambda: g.iota(o[0], pat, base, cm))
+
+    def iotaf(o, pat, base, cm):
+        emit("g", o[1], (), lambda: g.iota(o[0], pat, base, cm, allow_small_or_imprecise_dtypes=True))
+
+    def sel(o, i, pat, op, x, base, cm):
+        emit("g", o[1], i[1], lambda: g.affine_select(o[0], i[0], pat, op, x, base, cm))
 
     dma("s", T.DXI0[:, :], T.x[:, :], v("XI0")[1], ())
     dma("s", T.DENT[:, :], T.ent[:, :], v("ENT")[1], ())
@@ -178,143 +187,169 @@ def rank_program(g, core, T, topo):
             dma(q, to[:, lo:hi], frm[:, lo:hi], v(name, lo, hi)[1], ())
     dma("y", T.DTHI[:, :], T.th[:, :], v("THI")[1], ())
 
-    fill(v("REP0"), 1.0)
+    zb = v("W", 2432, 2944)
+    zf = v("IDS", 2400, 2544)
+
+    def zeros(n):
+        return v("W", 2432, 2432 + n)
+
+    fill(v("W", 2400, 2944), 0.0)
     fill(v("ONB"), 1.0)
-    iota(v("IP"), [[0, 256]], 0, 1)
-    iota(v("IC"), [[1, 256]], 0, 0)
-    emit("g", v("REP")[1], v("REP0")[1], lambda: g.affine_select(v("REP")[0], v("REP0")[0], [[1, 128], [0, 16]], A.is_equal, 0.0, 0, -1))
-    iota(v("I16"), [[0, 16], [1, 16]], 0, 0)
-    iota(v("IT"), [[16, 8], [1, 18]], -2, 0)
-    iota(v("IJ"), [[0, 8], [1, 18]], 0, 0)
-    iota(v("IA"), [[18, 8]], 17, 0)
-    iota(v("IS"), [[16, 16]], 0, 0)
-    iota(v("IK"), [[16, 8], [1, 12]], 0, 0)
-    iota(v("IB12"), [[12, 32]], 11, 0)
-    tt(v("IDB"), v("IP", 0, 128), v("IC", 0, 128), A.is_equal)
-    ts(v("GRP"), v("IP"), 4, A.arith_shift_right)
-    tt(v("ALF"), v("GRP", 0, 8), v("IC", 0, 8), A.is_equal)
-    ts(v("BETA"), v("IP"), 15, A.bitwise_and)
-    ts(v("BO"), v("ALF"), 128.0, A.mult)
-    tc(v("ZREP"), v("IC", 0, 48))
-    tc(v("IDF"), v("IDB"))
-    fill(v("CODE"), 0.0)
-    fill(v("ZB"), 0.0)
-    fill(v("RST"), 0.0)
-    fill(v("RST", 0, 144, 18), BIG)
-    fill(v("W", 2400, 4096), 0.0)
-    fill(v("W", 4088, 4096), 1024.0)
     fill(v("IDS", 2400, 2656), 0.0)
-    tc(v("ELU"), v("ENT"))
-    tc(v("ENTF"), v("ENT"))
+    iota(v("IP1"), [[0, 1]], 0, 1)
+    iotaf(v("J8"), [[1, 8]], 0, 0)
+    iota(v("IC"), [[1, 48]], 0, 0)
+    iota(v("IA"), [[18, 8]], 17, 0)
+    sel(v("IDB"), zeros(128), [[-1, 128]], A.not_equal, 1.0, 0, 1)
+    iotaf(v("I16"), [[0, 16], [1, 16]], 0, 0)
+    iota(v("IS"), [[16, 16]], 0, 0)
+    iota(v("IB12"), [[12, 32]], 11, 0)
+
+    def rep(sb):
+        sel(v("REP", 512 * sb, 512 * sb + 512), zb, [[-1, 32], [0, 16]], A.not_equal, 1.0, -32 * sb, 1)
+
+    def code(e):
+        iotaf(v("CODE", 288 * e, 288 * e + 144), [[0, 8], [1, 18]], 16 * e if e < 4 else 0, 0)
+
+    rep(0)
+    rep(1)
+    code(0)
+    sel(v("ADF"), zf, [[-16, 8], [-1, 18]], A.not_equal, 1.0, 2, 1)
+    sel(v("ADM"), zf, [[-16, 8], [-1, 18]], A.not_equal, 1.0, 1, 1)
+    rep(3)
+    rep(2)
+    for e in range(1, 5):
+        code(e)
+    iotaf(v("BLK"), [[0, 128]], 256, 0)
+    sel(v("BLK"), v("BLK"), [[-16, 8], [0, 16]], A.is_ge, 0.0, 0, 1)
+    sel(v("BLK"), v("BLK"), [[16, 8], [0, 16]], A.is_ge, 0.0, 15, -1)
+    iotaf(v("RC2"), [[0, 8], [1, 12]], 0, 0)
+    iotaf(v("KX"), [[1, 16], [16, 4]], 0, 0)
+    iotaf(v("ONF"), [[0, 128]], 1, 0)
+    for t in range(T_ - 1):
+        iotaf(v("XC%d" % t, 0, 96), [[0, 96]], -1, 0)
+    iotaf(v("NX", 256, 288), [[0, 32]], 65535, 0)
+    sel(v("TRI"), v("ONB", 0, 128), [[1, 128]], A.is_ge, 0.0, 0, -1)
+    sel(v("SEL"), zeros(96), [[-16, 8], [-1, 12]], A.not_equal, -4096.0, 0, 1)
+    for i, x in enumerate((0.75, 0.25, 0.875, 0.125, 0.5)):
+        sel(v("MIX", 128 * i, 128 * i + 128), zeros(128), [[-1, 128]], A.not_equal, x, 0, 1)
+    for i, x in enumerate((-3.0 / 1024, -7.0 / 2048, -1.0 / 512)):
+        sel(v("CB", 128 * i, 128 * i + 128), zeros(128), [[0, 128]], A.not_equal, x, 0, 0)
+    for i, x in enumerate((-2.0 ** 30, -2.0 ** 18)):
+        sel(v("BIGI", 128 * i, 128 * i + 128), zeros(128), [[-1, 128]], A.not_equal, x, 0, 1)
+    iotaf(v("RST12"), [[0, 384]], 0, 0)
+    sel(v("RST12"), v("RST12"), [[0, 32], [1, 12]], A.not_equal, BIG, 0, 0)
+    iotaf(v("PK", 2400, 2656), [[0, 256]], 65535, 0)
+
+    def prep_t(t, c):
+        mm(v("M1", 256, 384), v("XI0", 256 * t + 128 * c, 256 * t + 128 * c + 128), v("IDB"))
+
+    def prep_s(c):
+        act(v("XTN%d" % c), v("M1", 256, 384), F.Identity, scale=-1.0)
 
     def prep_x(t, c, blocks):
-        xtn = v("XTN%d" % c)
-        if 0 in blocks or c == 1:
-            mm(v("M1", 256, 384), v("XI0", 256 * t + 128 * c, 256 * t + 128 * c + 128), v("IDB"))
-            act(xtn, v("M1", 256, 384), F.Identity, scale=-1.0)
         for b in blocks:
             bank, sb, lo = v("M%d" % (b % 2)), (0, 1, 3)[b], 1536 * c + 512 * b
-            mm(bank, xtn, v("REP", 512 * sb, 512 * sb + 512))
+            mm(bank, v("XTN%d" % c), v("REP", 512 * sb, 512 * sb + 512))
             act(v("XR", lo, lo + 512), bank, F.Identity, scale=-1.0)
 
     def prep_l(t):
-        tt(v("ELX"), ind(v("ENTF", 16 * t, 16 * t + 16), v("ZREP", 0, 16)), v("MASK"), A.mult)
+        tt(v("ELX", 256 * t, 256 * t + 256), ind(v("ENTF", 16 * t, 16 * t + 16), v("ZREP", 0, 16)), v("MASK"), A.mult)
 
     def prep_e(t, lo):
-        mm(v("M1", lo, 256), v("BLK"), v("ELX", lo, 256), True, False)
+        mm(v("M1", lo, 256), v("BLK"), v("ELX", 256 * t + lo, 256 * t + 256), True, False)
         mm(v("M1", lo, 256), v("IDB"), v("XI0", 256 * t + lo, 256 * t + 256), False, True)
         act(v("XE", lo, 256), v("M1", lo, 256))
 
-    prep_x(0, 0, (0, 1, 2))
-    prep_x(0, 1, (0, 1, 2))
-    tt(v("MASK"), v("BETA"), v("I16"), A.is_equal)
-    tc(v("REPL"), v("IA"))
+    ts(v("GRP1"), v("IP1"), 4, A.arith_shift_right)
+    ts(v("BET1"), v("IP1"), 15, A.bitwise_and)
+    tc(v("GRPF"), v("GRP1"))
+    tc(v("BETF"), v("BET1"))
+    ts(v("ALF"), v("J8"), v("GRPF"), A.is_equal)
+    fill(v("RST"), 0.0)
+    fill(v("RST", 0, 144, 18), BIG)
+    fill(v("ZB"), 0.0)
     for e in range(5):
-        b = 288 * e
-        ts(v("CODE", b, b + 144), v("IJ"), float(16 * e if e < 4 else 0), A.add)
-        fill(v("CODE", b, b + 144, 18), 0.0 if e < 4 else FAR)
-        fill(v("CODE", b + 17, b + 144, 18), FAR)
-    ts(v("IT2"), v("IT"), 1.0, A.add)
-    tt(v("ADF"), v("IP", 0, 144), v("IT"), A.is_equal)
-    tt(v("ADM"), v("IP", 0, 144), v("IT2"), A.is_equal)
-    for n, j in (("ADF", 0), ("ADF", 1), ("ADM", 0), ("ADM", 17)):
-        fill(v(n, j, 144, 18), 0.0)
-    tt(v("ADF"), v("ADF"), v("ADM"), A.subtract)
-    ts(v("GC"), v("IC", 0, 128), 4, A.arith_shift_right)
-    tt(v("BLK"), v("GRP", 0, 128), v("GC"), A.is_equal)
-    ts(v("BLK"), v("BLK"), 256.0, A.mult)
+        fill(v("CODE", 288 * e + 144, 288 * e + 288), 0.0)
+    ts(v("MASK"), v("I16"), v("BETF"), A.is_equal)
+    tc(v("ZREP"), v("IC"))
+    tc(v("REPL"), v("IA"))
+    tc(v("ELU"), v("ENT"))
+    tc(v("ENTF"), v("ENT"))
     prep_l(0)
-    prep_e(0, 0)
+    fill(v("W", 2944, 4096), 0.0)
+    fill(v("W", 4088, 4096), 1024.0)
+    act(v("IDF"), v("IDB"))
+    act(v("BO"), v("ALF"), scale=128.0)
+    for c in range(2):
+        prep_t(0, c)
+        prep_s(c)
+        prep_x(0, c, (0, 1, 2))
+    for t in range(1, T_):
+        prep_l(t)
+    act(v("ALB"), v("ALF"))
+    act(v("WX"), v("ALF"), scale=2.0 ** 64)
+    for n, k in (("ALN", (1.0, -1.0, -1.0)), ("ALM", (0.0, -1.0, 1.0))):
+        for i, x in enumerate(k):
+            act(v(n, 8 * i, 8 * i + 8), v("ALF"), scale=x)
+    act(v("MASKB"), v("MASK"))
+    tc(v("K12R"), v("IB12"))
+    for i, k in ((0, 16.0), (1, 0.0)):
+        bi = v("BI%d" % i)
+        ts(bi, v("BETF"), float(i), A.is_equal)
+        ts(v("TA", 16 * i, 16 * i + 16), v("IC", 0, 16), k - 32.0, A.add)
+        ts(v("TA", 16 * i, 16 * i + 16), v("TA", 16 * i, 16 * i + 16), bi, A.mult)
+    tt(v("TB", 32, 48), v("TA", 0, 16), v("TA", 16, 32), A.add)
+    ts(v("NLST"), v("TB", 32, 48), 32.0, A.add)
+    fill(v("UVS", 32, 40), 0.0)
+    fill(v("HX", 256, 288), 0.0)
+    ts(v("TA", 64, 80), v("IS"), v("BETF"), A.add)
+    for n, lo, x in (("DUM", 0, 2656.0), ("DUM", 16, 2912.0), ("DZR", 0, 97.0)):
+        ts(v(n, lo, lo + 16), v("TA", 64, 80), x, A.add)
+    for per, top in ((16, 2.0 ** 62), (32, 0.8 * 2.0 ** 64)):
+        fill(v("TA", 0, 128), 0.25)
+        fill(v("TA", 0, 128, per), 0.0)
+        fill(v("TB", 0, 128), 0.0)
+        fill(v("TB", 0, 128, per), top)
+        scan(v("TA", 128, 256), v("TA", 0, 128), v("TB", 0, 128), 0.0, A.mult, A.add)
+        dg = v("TB", 128, 256) if per == 16 else v("NA", 0, 128)
+        tt(dg, v("TA", 128, 256), v("IDF"), A.mult)
+        if per == 16:
+            mm(v("L1", 0, 8), dg, v("ALF"))
+            act(v("WD0"), v("L1", 0, 8))
+            act(v("WD1"), v("L1", 0, 8), scale=2.0 ** -32)
+        else:
+            o, a = v("THC"), dg
+            emit("v", o[1], a[1], lambda: g.vector.tensor_reduce(out=o[0], in_=a[0], axis=AxisListType.X, op=A.add))
+    b1 = v("BETF")
+    ts(v("COLS", 3, 4), b1, 12.0, A.is_ge)
+    ts(v("COLS", 2, 3), v("COLS", 3, 4), -4096.0, A.mult, 36864.0, A.add)
+    ts(v("COLS", 6, 7), b1, 2.0, A.is_ge)
+    tt(v("COLS", 7, 8), v("COLS", 6, 7), v("COLS", 3, 4), A.subtract)
+    ts(v("COLS", 4, 5), v("COLS", 7, 8), 65535.0, A.mult)
+    for i, x in enumerate((980992.5 / 1048576, MAGIC, -MAGIC, 32768.0, -131072.0, 65535.0)):
+        fill(v("KC", i, i + 1), x)
+    ts(two("CR2", 0, 128), two("I16", 0, 128), 262144.0, A.mult)
+    ts(one("CR2", 0, 128), one("I16", 0, 128), 12.0, A.is_ge, 2.0 ** 31, A.mult)
+    ts(one("CR2", 0, 128), one("CR2", 0, 128), 2.0 ** 30, A.add)
+    fill(v("SEG"), 1.0)
+    fill(v("SEG", 0, 96, 16), 0.0)
+    tc(v("THF"), v("THI"))
+    ts(v("THA"), v("ALF"), v("THF"), A.mult, 8.0, A.mult)
+    mm(v("L1", 16, 24), v("ONF"), v("THA"))
+    act(v("TH128"), v("L1", 16, 24))
     for lo in (0, 1200):
         ts(v("NBM", lo, lo + 1200), v("NBI", lo, lo + 1200), 4095, A.bitwise_and)
         tc(v("IDS", lo, lo + 1200), v("NBM", lo, lo + 1200))
-
-    def late_constants():
-        fill(v("PK", 2400, 2656), 65535.0)
-        for lo in (0, 1200):
-            tc(v("PK", lo, lo + 1200), v("NBI", lo, lo + 1200))
-        tc(v("ALB"), v("ALF"))
-        for n, k in (("ALN", (1.0, -1.0, -1.0)), ("ALM", (0.0, -1.0, 1.0))):
-            for i, x in enumerate(k):
-                ts(v(n, 8 * i, 8 * i + 8), v("ALF"), x, A.mult)
-        tt(v("TRI"), v("IP", 0, 128), v("IC", 0, 128), A.is_le)
-        for i in range(3):
-            tc(v("MASKB", 256 * i, 256 * i + 256), v("MASK"))
-        for i, x in enumerate((262144.0, -262144.0)):
-            ts(v("BIGI", 128 * i, 128 * i + 128), v("IDB"), x, A.mult)
-        tt(v("SEL"), v("IP", 0, 96), v("IK"), A.is_equal)
-        fill(v("RST12"), 0.0)
-        fill(v("RST12", 0, 384, 12), BIG)
-        tc(v("K12R"), v("IB12"))
-        for i, k in ((0, 16.0), (1, 0.0)):
-            ts(v("TA", 16 * i, 16 * i + 16), v("IC", 0, 16), k - 32.0, A.add)
-            ts(v("TB", 16 * i, 16 * i + 16), v("BETA", 0, 16), float(i), A.is_equal)
-        tt(v("TA", 0, 32), v("TA", 0, 32), v("TB", 0, 32), A.mult)
-        tt(v("TB", 32, 48), v("TA", 0, 16), v("TA", 16, 32), A.add)
-        ts(v("NLST"), v("TB", 32, 48), 32.0, A.add)
-        fill(v("UVS", 32, 40), 0.0)
-        tt(v("TA", 64, 80), v("IS"), v("BETA", 0, 16), A.add)
-        for n, lo, x in (("DUM", 0, 2656.0), ("DUM", 16, 2912.0), ("DZN", 0, 801.0), ("DZR", 0, 97.0)):
-            ts(v(n, lo, lo + 16), v("TA", 64, 80), x, A.add)
-        for per, top in ((16, 2.0 ** 62), (32, 0.8 * 2.0 ** 64)):
-            fill(v("TA", 0, 128), 0.25)
-            fill(v("TA", 0, 128, per), 0.0)
-            fill(v("TB", 0, 128), 0.0)
-            fill(v("TB", 0, 128, per), top)
-            scan(v("TA", 128, 256), v("TA", 0, 128), v("TB", 0, 128), 0.0, A.mult, A.add)
-            tt(v("TB", 128, 256), v("TA", 128, 256), v("IDF"), A.mult)
-            if per == 16:
-                mm(v("M1", 0, 8), v("TB", 128, 256), v("ALF"))
-                tc(v("WD0"), v("M1", 0, 8))
-                ts(v("WD1"), v("WD0"), 2.0 ** -32, A.mult)
-                ts(v("WX"), v("ALF"), 2.0 ** 64, A.mult)
-            else:
-                o, a = v("THC"), v("TB", 128, 256)
-                emit("v", o[1], a[1], lambda: g.vector.tensor_reduce(out=o[0], in_=a[0], axis=AxisListType.X, op=A.add))
-        for i, x in enumerate((0.75, 0.25, 0.875, 0.125, 0.5)):
-            ts(v("MIX", 128 * i, 128 * i + 128), v("IDB"), x, A.mult)
-        for i, x in enumerate((-3.0 / 1024, -7.0 / 2048, -1.0 / 512)):
-            fill(v("CB", 128 * i, 128 * i + 128), x)
-        b1 = v("BETA", 0, 1)
-        ts(v("COLS", 3, 4), b1, 12.0, A.is_ge)
-        ts(v("COLS", 5, 6), v("COLS", 3, 4), 512.0, A.mult)
-        tt(v("COLS", 0, 1), v("COLS", 5, 6), b1, A.add)
-        ts(v("COLS", 1, 2), v("COLS", 3, 4), -1.0e20, A.mult, -2147418112.0, A.add)
-        ts(v("COLS", 2, 3), v("COLS", 3, 4), -4096.0, A.mult, 4096.0, A.add)
-        ts(v("COLS", 6, 7), b1, 2.0, A.is_ge)
-        tt(v("COLS", 7, 8), v("COLS", 6, 7), v("COLS", 3, 4), A.subtract)
-        ts(v("COLS", 4, 5), v("COLS", 7, 8), 65535.0, A.mult)
-        for i, x in enumerate((-2047.5 / 4096, MAGIC, 16 * (MAGIC + 9), 16.0, -131072.0)):
-            fill(v("KC", i, i + 1), x)
-        fill(v("SEG"), 1.0)
-        fill(v("SEG", 0, 96, 16), 0.0)
-        for t in range(T_ - 1):
-            fill(v("XC%d" % t, 0, 96), -1.0)
-        fill(v("ONF"), 1.0)
-        tc(v("THF"), v("THI"))
-        ts(v("THA"), v("ALF"), v("THF"), A.mult, 8.0, A.mult)
-        mm(v("M1", 16, 24), v("ONF"), v("THA"))
-        tc(v("TH128"), v("M1", 16, 24))
+    for e in range(5):
+        b = 288 * e
+        fill(v("CODE", b, b + 144, 18), 0.0 if e < 4 else FAR)
+        fill(v("CODE", b + 17, b + 144, 18), FAR)
+    for n, j in (("ADF", 0), ("ADF", 1), ("ADM", 0), ("ADM", 17)):
+        fill(v(n, j, 144, 18), 0.0)
+    tt(v("ADF"), v("ADF"), v("ADM"), A.subtract)
+    prep_e(0, 0)
+    fill(one("RC2", 0, 96), 4096.0)
 
     w_win, id_win, pk_win = v("W"), v("IDS", 0, 2656), v("PK", 0, 2656)
 
@@ -341,7 +376,7 @@ def rank_program(g, core, T, topo):
         gather_sub(c, 0)
         mm(v(k, 0, 287), one("ONB", 0, 128), one("CODE", 288 * e, 288 * e + 287), True, False)
         if e == 0:
-            mm(v(k, 144, 287, 18), v("ELX", 128 * c, 128 * c + 128), v("ALF"), False, False)
+            mm(v(k, 144, 287, 18), v("ELX", 256 * t + 128 * c, 256 * t + 128 * c + 128), v("ALF"), False, False)
         elif e < 4:
             mm(v(k, 0, 287, 18), v("IDF"), v("PU%d" % c, 17, 288, 18), False, False)
         absd(c, 0)
@@ -386,21 +421,22 @@ def rank_program(g, core, T, topo):
         if e < 4:
             tc(v("LUV", 8 * c, 8 * c + 8), v("L%d" % c, 0, 8))
         else:
+            tc(v("LUV", 16 + 8 * c, 24 + 8 * c), v("L%d" % c, 0, 8))
             rows(c, "PUV%d" % c, 1)
             act(v("NEGA", 8 * c, 8 * c + 8), v("L%d" % c, 8, 16))
             act(v("ABD", 8 * c, 8 * c + 8), v("L%d" % c, 16, 24), F.Abs)
-            tc(v("LUV", 16 + 8 * c, 24 + 8 * c), v("L%d" % c, 0, 8))
 
     def winners(c):
         tt(v("FARB", 8 * c, 8 * c + 8), v("PU%d" % c, 17, 144, 18), v("TH128"), A.is_ge)
         rows(c, "PU%d" % c, 0)
         act(v("UVS", 16 + 8 * c, 24 + 8 * c), v("PU%d" % c, 161, 288, 18))
-        act(v("EP", 128 * c, 128 * c + 128), ind(pk_win, v("LUV", 8 * c, 8 * c + 8)))
 
-    def put(name, t, src):
-        base = L_ + 64 * t
+    def put(name, src):
         scat(v(name, 0, 3168), v("OUV"), v(src, 0, 512))
-        scat(v(name, base, base + 1056), v("ON"), v(src, 512, 768))
+
+    def packed():
+        ts(v("N0", 256, 512), v("N0", 256, 512), 131071, A.bitwise_and)
+        put("PK", "N0")
 
     def merge(t):
         for j in range(3):
@@ -408,40 +444,52 @@ def rank_program(g, core, T, topo):
         ts(v("XM", 96, 192), v("XM", 0, 96), 255, A.bitwise_and)
         ts(v("XM", 192, 288), v("XM", 0, 96), 8, A.logical_shift_right, 4095, A.bitwise_and)
         tc(v("XI0", 256 * t + 160, 256 * t + 256), v("XM", 96, 192))
-        tt(v("ELX", 160, 256), v("XM", 192, 288), v("MASK", 160, 256), A.mult)
-        scan(v("OF", 0, 96), v("SEG"), v("ELX", 160, 256), 0.0, A.mult, A.add)
+        el = v("ELX", 256 * t + 160, 256 * t + 256)
+        tt(el, v("XM", 192, 288), v("MASK", 160, 256), A.mult)
+        scan(v("OF", 0, 96), v("SEG"), el, 0.0, A.mult, A.add)
         tc(v("ELU", 16 * t + 10, 16 * t + 16), v("OF", 15, 96, 16))
+        prep_t(t, 1)
+        prep_s(1)
         prep_x(t, 1, (1, 2))
-        prep_e(t, 160)
+        if t < T_ - 1:
+            prep_e(t, 160)
 
     def walks(t):
         prev = None
         for e in range(5):
             for c in range(2):
-                if t and e == 0 and c == 1:
-                    put("PK", t - 1, "NP")
-                    merge(t)
                 front1(t, e, c)
                 if prev:
                     post1(*prev)
+                if t and e == 0 and c == 0:
+                    merge(t)
                 front2(c)
+                if t and e == 0 and c == 0:
+                    packed()
                 if prev:
                     post2(*prev)
-                if t == 0 and e == 0 and c == 1:
-                    late_constants()
                 if e == 4:
                     winners(c)
                 prev = (e, c)
         post1(*prev)
-        count(range(4), 0)
+        count(t, range(4), 0)
         post2(*prev)
-        count(range(4, 8), 0)
-        count(range(8), 1)
-        count(range(8, 16), 1)
+        count(t, range(4, 8), 0)
+        count(t, range(8), 1)
+        count(t, range(8, 16), 1)
 
     nc = [0]
 
-    def count(blocks, rc):
+    def between(t, rc, a):
+        if rc == 0 and a < 4 and t == 0:
+            tc(v("PK", 600 * a, 600 * a + 600), v("NBI", 600 * a, 600 * a + 600))
+        for c in range(2):
+            if (rc, a) == (0, 4 + c):
+                tc(v("EPU", 128 * c, 128 * c + 128), ind(pk_win, v("LUV", 8 * c, 8 * c + 8)))
+            if (rc, a) == (1, c):
+                tc(v("EP", 256 + 128 * c, 384 + 128 * c), ind(pk_win, v("LUV", 16 + 8 * c, 24 + 8 * c)))
+
+    def count(t, blocks, rc):
         if blocks[0] == 0 and rc == 0:
             mm(v("K0", 480, 496), one("ONB", 0, 128), one("ZB", 0, 16), True, False)
         for a in blocks:
@@ -459,15 +507,9 @@ def rank_program(g, core, T, topo):
                 s0 = 2 * pr - lo
                 for x in range(2):
                     mm(v("K0", 480 + 8 * rc, 488 + 8 * rc, 1, pr + pn, pr), v(eq, s0 + x, s0 + 2 * pn, 2), v(wt), False, False)
+            between(t, rc, a)
         if blocks[-1] == 15:
             close("K0", 480, 496)
-
-    def offsets(lo, dz, out):
-        z, o, o2 = v("L0", lo, lo + 16), v("OF", lo, lo + 16), v("OF", lo + 64, lo + 80)
-        ts(o, z, 0.0, A.is_equal)
-        tt(o2, o, dz, A.mult)
-        tt(o, o2, z, A.add)
-        ts(out, o, -1.0, A.add)
 
     def lists(kind, lo):
         for c in range(2):
@@ -495,12 +537,26 @@ def rank_program(g, core, T, topo):
     def edit(t):
         last, base = t == T_ - 1, L_ + 64 * t
         vl = v("LUV", 16, 32)
-        act(v("EP", 256, 512), ind(pk_win, vl))
+        xs = v("XI0", 256 * t, 256 * t + 256)
+        wn, pn = v("W", base, base + 64), v("PK", base, base + 64)
+
+        def mix(bank, lo, a, f1, f2, k):
+            o = v(bank, lo, lo + 256)
+            mm(o, v("MIX", 128 * f1, 128 * f1 + 128), v("WUV", a, a + 256), True, False)
+            mm(o, v("MIX", 128 * f2, 128 * f2 + 128), xs, False, False)
+            mm(o, v("CB", 128 * k, 128 * k + 128), v("ONB"), False, True)
+
+        def slots():
+            for b in range(4):
+                k1, j = v("K1", 128 * b, 128 * b + 128), 128 * b
+                mm(k1, two("CR2", 0, 128), two("ONB", 0, 128), True, False)
+                mm(k1, v("BIGI", 0, 128), v("ZK", j, j + 128), False, False)
+                mm(k1, v("KR", j, j + 128), v("BIGI", 128, 256), False, False)
+                mm(k1, v("TGR", j, j + 128), v("IDF"), False, True)
+
+        act(v("AGE", 0, 256), v("EPU"), F.Identity, bias=v("KC", 0, 1), scale=2.0 ** -20)
         act(v("NGF", 256, 512), ind(id_win, vl))
-        act(v("AG"), v("EP"), F.Identity, bias=v("KC", 0, 1), scale=1.0 / 4096)
-        act(v("AH"), v("AG"), F.Identity, bias=v("KC", 1, 2))
-        act(v("QA"), v("AH"), F.Relu, bias=v("KC", 2, 3), scale=-16.0)
-        act(v("QB"), v("QA"), F.Identity, bias=v("KC", 3, 4))
+        act(v("AGE", 256, 512), v("EP", 256, 512), F.Identity, bias=v("KC", 0, 1), scale=2.0 ** -20)
         for c in range(2):
             act(v("UVS", 8 * c, 8 * c + 8), v("PUV%d" % c, 161, 288, 18))
         act(v("WUV"), ind(w_win, v("LUV")))
@@ -511,87 +567,109 @@ def rank_program(g, core, T, topo):
         mm(v("L1", 8, 16), v("ONB", 0, 128), v("W2", 0, 8), False, False)
         mm(v("L1", 24, 32), v("ONB", 0, 128), v("W2", 16, 24), False, False)
         close("L1", 0, 32)
+        for c in range(2):
+            for y in range(2):
+                j = 256 * y + 128 * c
+                tt(v("K1", j, j + 128), v("NGF", j, j + 128), v("M%d" % c, 1 - y, 256, 2), A.is_equal)
         tc(v("LF"), v("LUV"))
         tt(v("UMD"), v("LF"), v("DUM"), A.subtract)
         ts(v("SPA"), v("L1", 0, 32), 64.0, A.is_le)
         tt(v("SPL"), v("SPA"), v("W2"), A.mult)
-        tt(v("Z", 16, 32), v("SPL", 0, 16), v("L1", 0, 16), A.mult)
+        tc(v("PC"), v("L1", 0, 16))
         ts(v("NBV"), v("L1", 0, 32), float(base - 1), A.add)
         if not last:
             tt(v("RES"), v("FARB"), v("SPL", 0, 16), A.subtract)
             mm(v("L1", 64, 80), v("TRI"), v("RES"), True, False)
             mm(v("L1", 72, 80), v("ONB", 0, 128), v("RES", 0, 8), False, False)
             close("L1", 64, 80)
-        for c in range(2):
-            for y in range(2):
-                j = 256 * y + 128 * c
-                tt(v("NEQ", j, j + 128), v("NGF", j, j + 128), v("M%d" % c, 1 - y, 256, 2), A.not_equal)
+        tt(v("ZK"), v("K1"), v("AGE"), A.max)
+        for b in range(4):
+            k0 = v("K0", 96 * b, 96 * b + 96)
+            mm(k0, v("ZK", 128 * b, 128 * b + 128), v("SEL"), True, False)
+            mm(k0, two("ONB", 0, 128), two("RC2", 0, 96), False, True)
+        tt(v("TG1"), v("NBV"), v("UVS", 0, 32), A.subtract)
+        tt(v("TG2"), v("SPL"), v("TG1"), A.mult)
+        tt(v("TG"), v("TG2"), v("UVS", 0, 32), A.add)
         if not last:
             ts(v("SN", 0, 16), v("L1", 64, 80), 96.0, A.is_le)
             tt(v("SN", 16, 32), v("SN", 0, 16), v("RES"), A.mult)
             tt(v("Z", 32, 48), v("SN", 16, 32), v("L1", 64, 80), A.mult)
-            tt(v("EXZ", 512, 768), ind(v("Z", 32, 48), v("ZREP", 0, 16)), v("MASKB", 512, 768), A.mult)
-            lists(2, 48)
-        tt(v("EXZ", 0, 512), ind(v("Z", 0, 32), v("ZREP", 0, 32)), v("MASKB", 0, 512), A.mult)
-        if not last:
-            offsets(48, v("DZR"), v("ORR"))
-            scat(v("XC%d" % t, 0, 352), v("ORR"), v("XE"), True)
-            send(t)
+            tt(v("EXZ", 256, 512), ind(v("Z", 32, 48), v("ZREP", 0, 16)), v("MASKB"), A.mult)
+            lists(1, 48)
+        tt(v("EXZ", 0, 256), ind(v("Z", 0, 16), v("ZREP", 0, 16)), v("MASKB"), A.mult)
         lists(0, 0)
         lists(0, 16)
-        lists(1, 32)
-        tt(v("ZK"), v("NEQ"), v("QB"), A.mult)
-        act(v("KS"), v("ZK"), F.Identity, bias=v("COLS", 0, 1))
-        for b in range(4):
-            mm(v("K0", 96 * b, 96 * b + 96), v("KS", 128 * b, 128 * b + 128), v("SEL"))
-        tt(v("TG1"), v("NBV"), v("UVS", 0, 32), A.subtract)
-        tt(v("TG2"), v("SPL"), v("TG1"), A.mult)
-        tt(v("TG"), v("TG2"), v("UVS", 0, 32), A.add)
-        act(v("TGR"), ind(v("TG"), v("ZREP", 0, 32)), F.Identity, bias=v("KC", 4, 5))
-        xs = v("XI0", 256 * t, 256 * t + 256)
-        for bank, lo, a, f1, f2, k in (("S1", 0, 0, 0, 1, 0), ("S1", 256, 256, 2, 3, 1), ("S0", 0, 0, 4, 4, 2)):
-            o = v(bank, lo, lo + 256)
-            mm(o, v("MIX", 128 * f1, 128 * f1 + 128), v("WUV", a, a + 256), True, False)
-            mm(o, v("MIX", 128 * f2, 128 * f2 + 128), xs, False, False)
-            mm(o, v("CB", 128 * k, 128 * k + 128), v("ONB"), False, True)
+        mix("S1", 0, 0, 0, 1, 0)
+        mix("S1", 256, 256, 2, 3, 1)
         scan(v("KM"), v("RST12"), v("K0", 0, 384), BIG, A.max, A.min)
+        act(v("TGR", 0, 256), ind(v("TG"), v("ZREP", 0, 16)))
+        act(v("TGR", 256, 512), ind(v("TG"), v("ZREP", 16, 32)), F.Identity, bias=v("KC", 4, 5))
+        act(v("T1"), v("EPU"), F.Relu, bias=v("KC", 3, 4), scale=-1.0)
         act(v("KR"), ind(v("KM"), v("K12R")))
-        for b in range(4):
-            k1, j = v("K1", 128 * b, 128 * b + 128), 128 * b
-            mm(k1, v("BIGI", 0, 128), v("KS", j, j + 128), True, False)
-            mm(k1, v("KR", j, j + 128), v("BIGI", 128, 256), False, False)
-            mm(k1, v("TGR", j, j + 128), v("IDF"), False, True)
+        if not last:
+            slots()
+            z, o, o2 = v("L0", 48, 64), v("OF", 48, 64), v("OF", 112, 128)
+            ts(o, z, 0.0, A.is_equal)
+            tt(o2, o, v("DZR"), A.mult)
+            tt(o, o2, z, A.add)
+            ts(v("ORR"), o, -1.0, A.add)
+            scat(v("XC%d" % t, 0, 352), v("ORR"), v("XE"), True)
+            send(t)
         tt(v("OF", 128, 160), v("L0", 0, 32), v("UMD"), A.mult)
         tt(v("OF", 160, 192), v("OF", 128, 160), v("DUM"), A.add)
         tc(v("OUV"), v("OF", 160, 192))
-        offsets(32, v("DZN"), v("ON"))
-        tc(v("WNI", 0, 512), v("S1"))
-        tc(v("WNI", 512, 768), v("S0", 0, 256))
-        act(v("T1"), v("EP", 0, 256), F.Relu, bias=v("COLS", 1, 2), scale=65536.0)
-        act(v("NA"), v("EP", 0, 256), F.Identity, bias=v("COLS", 4, 5), scale=v("COLS", 3, 4))
         for c in range(2):
-            nr2 = v("NR2", 128 * c, 128 * c + 128)
-            act(nr2, ind(v("UVS"), v("NLST", 8 * c, 8 * c + 8)))
-            mm(v("L1", 256 + 128 * c, 384 + 128 * c), nr2, v("IDF"))
+            for k in range(8):
+                ts(v("C%d" % c, 64 * k, 64 * k + 64), v("KX"), v("PC", 8 * c + k, 8 * c + k + 1), A.is_ge)
         if not last:
-            prep_l(t + 1)
-            prep_x(t + 1, 0, (0, 1, 2))
-            prep_e(t + 1, 0)
-            prep_x(t + 1, 1, (0,))
-        put("W", t, "WNI")
+            prep_t(t + 1, 0)
+        for a in range(4):
+            for c in range(2):
+                mm(v("L0", 32 + a, 33 + a), v("C%d" % c, a, 512, 4), v("ONB", 0, 1), c == 0, c == 1)
+        act(v("R1", 0, 512), v("S1"), F.Identity, bias=v("KC", 1, 2))
+        act(v("WNB"), v("R1", 0, 512), F.Identity, bias=v("KC", 2, 3))
+        put("W", "WNB")
+        act(v("AQ"), v("T1"), F.Identity, bias=v("COLS", 2, 3), scale=-1.0)
+        act(v("S1", 0, 256), v("T1"), F.Relu, bias=v("KC", 5, 6), scale=-65535.0)
+        for c in range(2):
+            act(v("NR2", 128 * c, 128 * c + 128), ind(v("UVS"), v("NLST", 8 * c, 8 * c + 8)))
+        act(v("NA"), v("EPU"), F.Identity, bias=v("COLS", 4, 5), scale=v("COLS", 3, 4))
+        if not last:
+            prep_s(0)
+            prep_x(t + 1, 0, (0, 1))
+        mix("S0", 0, 0, 4, 4, 2)
+        act(v("R1", 512, 768), v("S0", 0, 256), F.Identity, bias=v("KC", 1, 2))
+        act(v("HX", 0, 256), v("R1", 512, 768), F.Identity, bias=v("KC", 2, 3))
         if last:
+            slots()
+        for c in range(2):
+            mm(v("L1", 256 + 128 * c, 384 + 128 * c), v("NR2", 128 * c, 128 * c + 128), v("IDF"))
+        if not last:
+            prep_x(t + 1, 0, (2,))
+            prep_t(t + 1, 1)
+            prep_s(1)
+            prep_e(t + 1, 0 if t + 1 < T_ - 1 else 160)
+            prep_x(t + 1, 1, (0,))
+        if last:
+            tc(v("NL"), v("L0", 32, 36))
+            tc(wn, ind(v("HX", 0, 257), v("NL")))
             for lo, hi, q in ((0, 1328, "y"), (1328, 2656, "s")):
                 dma(q, T.yw[:, lo:hi], T.W[:, lo:hi], (), v("W", lo, hi)[1])
-        tt(v("E1"), v("EP", 0, 256), v("T1"), A.add)
-        ts(v("EP", 0, 256), v("E1"), v("COLS", 2, 3), A.add, 65535.0, A.min)
-        tt(v("N0", 512, 768), v("NA"), v("L1", 256, 512), A.add)
-        tt(v("N0", 0, 512), v("EP"), v("K1"), A.min)
+        tt(v("EP", 0, 256), v("AQ"), v("S1", 0, 256), A.max)
+        tt(v("N0"), v("EP"), v("K1"), A.min)
         if not last:
             ts(v("NI"), v("N0"), 4095, A.bitwise_and)
-            put("IDS", t, "NI")
-        ts(v("NP"), v("N0"), 131071, A.bitwise_and)
-        if last:
-            put("PK", t, "NP")
+            put("IDS", "NI")
+            tc(v("NL"), v("L0", 32, 36))
+            tc(wn, ind(v("HX", 0, 257), v("NL")))
+        tt(v("NX", 0, 256), v("NA"), v("L1", 256, 512), A.add)
+        tc(pn, ind(v("NX", 0, 257), v("NL")))
+        if not last:
+            tc(v("QI"), pn)
+            ts(v("QI"), v("QI"), 4095, A.bitwise_and)
+            tc(v("IDS", base, base + 64), v("QI"))
+        else:
+            packed()
             for lo, hi, q in ((0, 1328, "y"), (1328, 2656, "s")):
                 dma(q, T.yn[:, lo:hi], T.PK[:, lo:hi], (), v("PK", lo, hi)[1])
 

from concourse.bass import DstId, RemoteDMATransfer
from concourse.mybir import dt, AluOpType, AxisListType, ActivationFunctionType

A = AluOpType
F = ActivationFunctionType
T_, NB_, L_, BIG = 4, 4, 2400, 1.0e9
FAR = 8388608.0
MAGIC = 12582912.0
_S = {}
for _d, _l in (
        ("bfloat16", "W 4096 XI0 1024 MASKB 256 IDB 128 ALB 8 BO 8 TRI 128 ONB 256 SEL 96 ZB 288 CODE 1440 WD0 8 WD1 8 WX 8 REP 2048 MIX 640 CB 384 BIGI 256 "
         "XR 3072 FARB 16 WUV 512 Z 48 W2 32 SPA 32 SPL 32 RES 16 SN 32 EXZ 512 EQ0 256 EQ1 256 EQ2 256 EQ3 256 "
         "AGE 512 ZK 512 KR 512 I16 256 J8 8 KX 64 CR2 128 RC2 96 C0 512 C1 512 WNB 512"),
        ("float32", "IDS 3168 PK 3168 ENTF 64 THF 1 THA 8 MASK 256 IDF 128 ALF 8 ALN 24 ALM 24 ONF 128 ADF 144 ADM 144 RST 144 RST12 384 DUM 32 DZR 16 "
         "THC 1 TH128 8 BLK 128 COLS 8 KC 8 SEG 96 TA 256 TB 256 XE 256 ELX 1024 NGF 512 NEGA 16 ABD 16 UVS 40 LF 32 UMD 32 EP 512 EPU 256 NBV 32 TG1 32 TG2 32 TG 32 "
         "OF 192 KM 384 T1 256 AQ 256 TGR 512 NR2 256 NA 256 NX 288 HX 288 R1 768 PC 16 AB0 256 AB1 256 AB2 256 GRPF 1 BETF 1 BI0 1 BI1 1"),
        ("int32", "NBI 2400 NBM 2400 ENT 64 THI 1 IP1 1 GRP1 1 BET1 1 IC 48 IA 8 IB12 32 IS 16 N0 512 NI 512 XM 288 QI 64"),
        ("uint16", "ELU 64 REPL 8 ZREP 48 K12R 32 NLST 16 LUV 32 OUV 32 ORR 16 NL 4")):
    _l = _l.split()
    for _i in range(0, len(_l), 2):
        _S[_l[_i]] = (int(_l[_i + 1]), _d)
for _c in range(2):
    for _n, _w, _d in (("NGU", 128, "uint16"), ("GS", 512, "bfloat16"), ("DV", 1536, "bfloat16"), ("AD", 2048, "bfloat16"), ("D0", 128, "bfloat16"), ("A0", 128, "bfloat16"),
                       ("PU", 288, "float32"), ("NR", 144, "float32"), ("EX", 128, "float32"), ("PUV", 288, "float32"),
                       ("EXV", 128, "float32"), ("RU", 128, "float32"), ("XTN", 128, "bfloat16")):
        _S[_n + str(_c)] = (_w, _d)
SCRATCH, _PACK, _WIDTH = {}, {}, {"float32": 0, "bfloat16": 0, "int32": 0, "uint16": 0}
for _n, (_w, _d) in _S.items():
    if _n in ("XI0", "ENT", "THI"):
        SCRATCH["D" + _n] = ("sbuf", [128, _w], _d)
        _PACK[_n] = ("D" + _n, 0)
    elif _w <= 768:
        _PACK[_n] = ("A" + _d, _WIDTH[_d])
        _WIDTH[_d] += (_w + 31) // 32 * 32
    else:
        SCRATCH[_n] = ("sbuf", [128, _w], _d)
for _d, _w in _WIDTH.items():
    SCRATCH["A" + _d] = ("sbuf", [128, _w], _d)
for _t in range(T_ - 1):
    SCRATCH["XC%d" % _t] = ("sbuf", [128, 352], "float32")
    for _j in range(3):
        SCRATCH["RX%d_%d" % (_t, _j)] = ("sbuf", [128, 96], "float32")
_BANKS = ("K0", "K1", "S0", "S1", "L0", "L1", "M0", "M1")
for _n in _BANKS:
    SCRATCH[_n] = ("psum", [128, 512], "float32")
_ENG = {"v": "sv", "s": "ss", "t": "st", "g": "sg"}
SEMAPHORES = list(_ENG.values()) + ["dm%d" % i for i in range(12)] + ["rx%d_%d" % (t, j) for t in range(3) for j in range(3)] + ["lx%d" % t for t in range(3)]


def rank_program(g, core, T, topo):
    rank = T.rank_of(core)
    if rank is None:
        return
    qs = {"v": g.vector, "s": g.scalar, "t": g.tensor, "g": g, "y": g.sync}
    cnt = {}
    known = {q: {} for q in qs}
    hist = {}
    unit = {}
    acc = {}
    for e, s in _ENG.items():
        unit[e] = (T.sem[s], 1)

    def v(name, lo=0, hi=None, st=1, p1=128, p0=0):
        hi = hi if hi is not None else (_S[name][0] if name in _S else 512)
        buf, off = _PACK[name] if name in _PACK else (name, 0)
        ap = T[buf][p0:p1, lo + off:hi + off] if st == 1 else T[buf][p0:p1, lo + off:hi + off:st]
        n = (hi - lo + st - 1) // st
        return (ap, ((buf, off + lo, off + lo + (n - 1) * st + 1, p0, p1, st),))

    def ind(w, o):
        return (w[0].indirect(o[0]), w[1] + o[1])

    def wait(q, src, i):
        if known[q].get(src, 0) >= i:
            return
        sem, step = unit[src]
        qs[q].wait_ge(sem, i * step)
        for k, n in hist[(src, i)].items():
            if known[q].get(k, 0) < n:
                known[q][k] = n
        known[q][src] = max(i, known[q].get(src, 0))

    def access(q, src, outs, ins):
        need = {}
        for regs, wr in ((ins, False), (outs, True)):
            for (b, lo, hi, p0, p1, st) in regs:
                for (s2, i2, lo2, hi2, a0, a1, st2, w2) in acc.get(b, ()):
                    if s2 == q == "t":
                        continue
                    if b in _BANKS and s2 != q:
                        pass
                    elif not (wr or w2) or lo2 >= hi or lo >= hi2 or a0 >= p1 or p0 >= a1:
                        continue
                    if need.get(s2, 0) < i2:
                        need[s2] = i2
        for s2 in sorted(need, key=lambda k: -len(hist[(k, need[k])])):
            wait(q, s2, need[s2])
        i = cnt.get(src, 0) + 1
        cnt[src] = i
        hist[(src, i)] = dict(known[q])
        for regs, wr in ((ins, False), (outs, True)):
            for (b, lo, hi, p0, p1, st) in regs:
                keep = []
                for r in acc.get(b, ()):
                    if wr and st == 1 and lo <= r[2] and r[3] <= hi and p0 <= r[4] and r[5] <= p1:
                        continue
                    if r[0] == src and r[7] == wr and r[2:6] == (lo, hi, p0, p1):
                        continue
                    keep.append(r)
                keep.append((src, i, lo, hi, p0, p1, st, wr))
                acc[b] = keep

    def emit(q, outs, ins, call):
        access(q, q, outs, ins)
        call().then_inc(unit[q][0], 1)

    nd = [0]

    def dma(q, out, in_, outs, ins):
        src = "d%d" % nd[0]
        unit[src] = (T.sem["dm%d" % nd[0]], 16)
        nd[0] += 1
        access(q, src, outs, ins)
        qs[q].dma_start(out=out, in_=in_).then_inc(unit[src][0], 16)

    def tt(o, a, b, op):
        emit("v", o[1], a[1] + b[1], lambda: g.vector.tensor_tensor(out=o[0], in0=a[0], in1=b[0], op=op))

    def ts(o, a, s1, op0, s2=None, op1=None):
        ins, x1 = a[1], s1
        if isinstance(s1, tuple):
            ins, x1 = ins + s1[1], s1[0]
        if op1 is None:
            emit("v", o[1], ins, lambda: g.vector.tensor_scalar(out=o[0], in0=a[0], scalar1=x1, scalar2=None, op0=op0))
        else:
            emit("v", o[1], ins, lambda: g.vector.tensor_scalar(out=o[0], in0=a[0], scalar1=x1, scalar2=s2, op0=op0, op1=op1))

    def tc(o, a):
        emit("v", o[1], a[1], lambda: g.vector.tensor_copy(out=o[0], in_=a[0]))

    def scat(w, o, a, flag=False):
        if flag:
            emit("v", w[1], o[1] + a[1], lambda: g.vector.tensor_scalar(out=w[0].indirect(o[0]), in0=a[0], scalar1=1.0, scalar2=1048576.0, op0=A.mult, op1=A.add))
        else:
            emit("v", w[1], o[1] + a[1], lambda: g.vector.tensor_copy(out=w[0].indirect(o[0]), in_=a[0]))

    def scan(o, d0, d1, init, op0, op1):
        emit("v", o[1], d0[1] + d1[1], lambda: g.vector.tensor_tensor_scan(out=o[0], data0=d0[0], data1=d1[0], initial=init, op0=op0, op1=op1))

    def fill(o, x):
        emit("v", o[1], (), lambda: g.vector.memset(o[0], x))

    def act(o, a, f=F.Copy, bias=None, scale=None):
        ins, kw = a[1], {}
        for k, x in (("bias", bias), ("scale", scale)):
            if isinstance(x, tuple):
                ins, kw[k] = ins + x[1], x[0]
            elif x is not None:
                kw[k] = x
        emit("s", o[1], ins, lambda: g.scalar.activation(out=o[0], in_=a[0], func=f, **kw))

    def mm(o, l, r, start=True, stop=True):
        emit("t", o[1], l[1] + r[1], lambda: g.tensor.matmul(out=o[0], lhsT=l[0], rhs=r[0], start=start, stop=stop))

    def one(name, lo, hi):
        return v(name, lo, hi, 1, 1)

    def two(name, lo, hi):
        return v(name, lo, hi, 1, 2)

    def close(name, lo, hi):
        mm(v(name, lo, hi), one("ONB", 0, 128), one("ZB", 0, hi - lo), False, True)

    def iota(o, pat, base, cm):
        emit("g", o[1], (), lambda: g.iota(o[0], pat, base, cm))

    def iotaf(o, pat, base, cm):
        emit("g", o[1], (), lambda: g.iota(o[0], pat, base, cm, allow_small_or_imprecise_dtypes=True))

    def sel(o, i, pat, op, x, base, cm):
        emit("g", o[1], i[1], lambda: g.affine_select(o[0], i[0], pat, op, x, base, cm))

    dma("s", T.DXI0[:, :], T.x[:, :], v("XI0")[1], ())
    dma("s", T.DENT[:, :], T.ent[:, :], v("ENT")[1], ())
    for to, frm, name in ((T.NBI, T.nb, "NBI"), (T.W, T.w, "W")):
        for lo, hi, q in ((0, 1200, "y"), (1200, 2400, "s")):
            dma(q, to[:, lo:hi], frm[:, lo:hi], v(name, lo, hi)[1], ())
    dma("y", T.DTHI[:, :], T.th[:, :], v("THI")[1], ())

    zb = v("W", 2432, 2944)
    zf = v("IDS", 2400, 2544)

    def zeros(n):
        return v("W", 2432, 2432 + n)

    fill(v("W", 2400, 2944), 0.0)
    fill(v("ONB"), 1.0)
    fill(v("IDS", 2400, 2656), 0.0)
    iota(v("IP1"), [[0, 1]], 0, 1)
    iotaf(v("J8"), [[1, 8]], 0, 0)
    iota(v("IC"), [[1, 48]], 0, 0)
    iota(v("IA"), [[18, 8]], 17, 0)
    sel(v("IDB"), zeros(128), [[-1, 128]], A.not_equal, 1.0, 0, 1)
    iotaf(v("I16"), [[0, 16], [1, 16]], 0, 0)
    iota(v("IS"), [[16, 16]], 0, 0)
    iota(v("IB12"), [[12, 32]], 11, 0)

    def rep(sb):
        sel(v("REP", 512 * sb, 512 * sb + 512), zb, [[-1, 32], [0, 16]], A.not_equal, 1.0, -32 * sb, 1)

    def code(e):
        iotaf(v("CODE", 288 * e, 288 * e + 144), [[0, 8], [1, 18]], 16 * e if e < 4 else 0, 0)

    rep(0)
    rep(1)
    code(0)
    sel(v("ADF"), zf, [[-16, 8], [-1, 18]], A.not_equal, 1.0, 2, 1)
    sel(v("ADM"), zf, [[-16, 8], [-1, 18]], A.not_equal, 1.0, 1, 1)
    rep(3)
    rep(2)
    for e in range(1, 5):
        code(e)
    iotaf(v("BLK"), [[0, 128]], 256, 0)
    sel(v("BLK"), v("BLK"), [[-16, 8], [0, 16]], A.is_ge, 0.0, 0, 1)
    sel(v("BLK"), v("BLK"), [[16, 8], [0, 16]], A.is_ge, 0.0, 15, -1)
    iotaf(v("RC2"), [[0, 8], [1, 12]], 0, 0)
    iotaf(v("KX"), [[1, 16], [16, 4]], 0, 0)
    iotaf(v("ONF"), [[0, 128]], 1, 0)
    for t in range(T_ - 1):
        iotaf(v("XC%d" % t, 0, 96), [[0, 96]], -1, 0)
    iotaf(v("NX", 256, 288), [[0, 32]], 65535, 0)
    sel(v("TRI"), v("ONB", 0, 128), [[1, 128]], A.is_ge, 0.0, 0, -1)
    sel(v("SEL"), zeros(96), [[-16, 8], [-1, 12]], A.not_equal, -4096.0, 0, 1)
    for i, x in enumerate((0.75, 0.25, 0.875, 0.125, 0.5)):
        sel(v("MIX", 128 * i, 128 * i + 128), zeros(128), [[-1, 128]], A.not_equal, x, 0, 1)
    for i, x in enumerate((-3.0 / 1024, -7.0 / 2048, -1.0 / 512)):
        sel(v("CB", 128 * i, 128 * i + 128), zeros(128), [[0, 128]], A.not_equal, x, 0, 0)
    for i, x in enumerate((-2.0 ** 30, -2.0 ** 18)):
        sel(v("BIGI", 128 * i, 128 * i + 128), zeros(128), [[-1, 128]], A.not_equal, x, 0, 1)
    iotaf(v("RST12"), [[0, 384]], 0, 0)
    sel(v("RST12"), v("RST12"), [[0, 32], [1, 12]], A.not_equal, BIG, 0, 0)
    iotaf(v("PK", 2400, 2656), [[0, 256]], 65535, 0)

    def prep_t(t, c):
        mm(v("M1", 256, 384), v("XI0", 256 * t + 128 * c, 256 * t + 128 * c + 128), v("IDB"))

    def prep_s(c):
        act(v("XTN%d" % c), v("M1", 256, 384), F.Identity, scale=-1.0)

    def prep_x(t, c, blocks):
        for b in blocks:
            bank, sb, lo = v("M%d" % (b % 2)), (0, 1, 3)[b], 1536 * c + 512 * b
            mm(bank, v("XTN%d" % c), v("REP", 512 * sb, 512 * sb + 512))
            act(v("XR", lo, lo + 512), bank, F.Identity, scale=-1.0)

    def prep_l(t):
        tt(v("ELX", 256 * t, 256 * t + 256), ind(v("ENTF", 16 * t, 16 * t + 16), v("ZREP", 0, 16)), v("MASK"), A.mult)

    def prep_e(t, lo):
        mm(v("M1", lo, 256), v("BLK"), v("ELX", 256 * t + lo, 256 * t + 256), True, False)
        mm(v("M1", lo, 256), v("IDB"), v("XI0", 256 * t + lo, 256 * t + 256), False, True)
        act(v("XE", lo, 256), v("M1", lo, 256))

    ts(v("GRP1"), v("IP1"), 4, A.arith_shift_right)
    ts(v("BET1"), v("IP1"), 15, A.bitwise_and)
    tc(v("GRPF"), v("GRP1"))
    tc(v("BETF"), v("BET1"))
    ts(v("ALF"), v("J8"), v("GRPF"), A.is_equal)
    fill(v("RST"), 0.0)
    fill(v("RST", 0, 144, 18), BIG)
    fill(v("ZB"), 0.0)
    for e in range(5):
        fill(v("CODE", 288 * e + 144, 288 * e + 288), 0.0)
    ts(v("MASK"), v("I16"), v("BETF"), A.is_equal)
    tc(v("ZREP"), v("IC"))
    tc(v("REPL"), v("IA"))
    tc(v("ELU"), v("ENT"))
    tc(v("ENTF"), v("ENT"))
    prep_l(0)
    fill(v("W", 2944, 4096), 0.0)
    fill(v("W", 4088, 4096), 1024.0)
    act(v("IDF"), v("IDB"))
    act(v("BO"), v("ALF"), scale=128.0)
    for c in range(2):
        prep_t(0, c)
        prep_s(c)
        prep_x(0, c, (0, 1, 2))
    for t in range(1, T_):
        prep_l(t)
    act(v("ALB"), v("ALF"))
    act(v("WX"), v("ALF"), scale=2.0 ** 64)
    for n, k in (("ALN", (1.0, -1.0, -1.0)), ("ALM", (0.0, -1.0, 1.0))):
        for i, x in enumerate(k):
            act(v(n, 8 * i, 8 * i + 8), v("ALF"), scale=x)
    act(v("MASKB"), v("MASK"))
    tc(v("K12R"), v("IB12"))
    for i, k in ((0, 16.0), (1, 0.0)):
        bi = v("BI%d" % i)
        ts(bi, v("BETF"), float(i), A.is_equal)
        ts(v("TA", 16 * i, 16 * i + 16), v("IC", 0, 16), k - 32.0, A.add)
        ts(v("TA", 16 * i, 16 * i + 16), v("TA", 16 * i, 16 * i + 16), bi, A.mult)
    tt(v("TB", 32, 48), v("TA", 0, 16), v("TA", 16, 32), A.add)
    ts(v("NLST"), v("TB", 32, 48), 32.0, A.add)
    fill(v("UVS", 32, 40), 0.0)
    fill(v("HX", 256, 288), 0.0)
    ts(v("TA", 64, 80), v("IS"), v("BETF"), A.add)
    for n, lo, x in (("DUM", 0, 2656.0), ("DUM", 16, 2912.0), ("DZR", 0, 97.0)):
        ts(v(n, lo, lo + 16), v("TA", 64, 80), x, A.add)
    for per, top in ((16, 2.0 ** 62), (32, 0.8 * 2.0 ** 64)):
        fill(v("TA", 0, 128), 0.25)
        fill(v("TA", 0, 128, per), 0.0)
        fill(v("TB", 0, 128), 0.0)
        fill(v("TB", 0, 128, per), top)
        scan(v("TA", 128, 256), v("TA", 0, 128), v("TB", 0, 128), 0.0, A.mult, A.add)
        dg = v("TB", 128, 256) if per == 16 else v("NA", 0, 128)
        tt(dg, v("TA", 128, 256), v("IDF"), A.mult)
        if per == 16:
            mm(v("L1", 0, 8), dg, v("ALF"))
            act(v("WD0"), v("L1", 0, 8))
            act(v("WD1"), v("L1", 0, 8), scale=2.0 ** -32)
        else:
            o, a = v("THC"), dg
            emit("v", o[1], a[1], lambda: g.vector.tensor_reduce(out=o[0], in_=a[0], axis=AxisListType.X, op=A.add))
    b1 = v("BETF")
    ts(v("COLS", 3, 4), b1, 12.0, A.is_ge)
    ts(v("COLS", 2, 3), v("COLS", 3, 4), -4096.0, A.mult, 36864.0, A.add)
    ts(v("COLS", 6, 7), b1, 2.0, A.is_ge)
    tt(v("COLS", 7, 8), v("COLS", 6, 7), v("COLS", 3, 4), A.subtract)
    ts(v("COLS", 4, 5), v("COLS", 7, 8), 65535.0, A.mult)
    for i, x in enumerate((980992.5 / 1048576, MAGIC, -MAGIC, 32768.0, -131072.0, 65535.0)):
        fill(v("KC", i, i + 1), x)
    ts(two("CR2", 0, 128), two("I16", 0, 128), 262144.0, A.mult)
    ts(one("CR2", 0, 128), one("I16", 0, 128), 12.0, A.is_ge, 2.0 ** 31, A.mult)
    ts(one("CR2", 0, 128), one("CR2", 0, 128), 2.0 ** 30, A.add)
    fill(v("SEG"), 1.0)
    fill(v("SEG", 0, 96, 16), 0.0)
    tc(v("THF"), v("THI"))
    ts(v("THA"), v("ALF"), v("THF"), A.mult, 8.0, A.mult)
    mm(v("L1", 16, 24), v("ONF"), v("THA"))
    act(v("TH128"), v("L1", 16, 24))
    for lo in (0, 1200):
        ts(v("NBM", lo, lo + 1200), v("NBI", lo, lo + 1200), 4095, A.bitwise_and)
        tc(v("IDS", lo, lo + 1200), v("NBM", lo, lo + 1200))
    for e in range(5):
        b = 288 * e
        fill(v("CODE", b, b + 144, 18), 0.0 if e < 4 else FAR)
        fill(v("CODE", b + 17, b + 144, 18), FAR)
    for n, j in (("ADF", 0), ("ADF", 1), ("ADM", 0), ("ADM", 17)):
        fill(v(n, j, 144, 18), 0.0)
    tt(v("ADF"), v("ADF"), v("ADM"), A.subtract)
    prep_e(0, 0)
    fill(one("RC2", 0, 96), 4096.0)

    w_win, id_win, pk_win = v("W"), v("IDS", 0, 2656), v("PK", 0, 2656)

    def gather_sub(c, b):
        sb = (0, 1, 3)[b]
        tt(v("DV%d" % c, 512 * b, 512 * b + 512), ind(w_win, v("NGU%d" % c, 32 * sb, 32 * sb + 32)),
           v("XR", 1536 * c + 512 * b, 1536 * c + 512 * b + 512), A.subtract)

    def absd(c, sb):
        src = v("S%d" % c) if sb == 2 else v("DV%d" % c, 512 * min(sb, 2), 512 * min(sb, 2) + 512)
        act(v("AD%d" % c, 512 * sb, 512 * sb + 512), src, F.Abs)

    def dist(c, b0, b1):
        for i in range(16):
            mm(v("K%d" % c, 1 + i, 144, 18, 32 * b1, 32 * b0), v("AD%d" % c, 512 * b0 + i, 512 * b1, 16), v("BO"), False, False)

    def front1(t, e, c):
        k = "K%d" % c
        ul = v("ELU", 16 * t + 8 * c, 16 * t + 8 * c + 8) if e == 0 else v("LUV", 8 * c, 8 * c + 8)
        ngf = v("NGF", 128 * c, 128 * c + 128)
        tc(v("NGU%d" % c), ind(id_win, ul))
        act(ngf, ind(id_win, ul))
        act(v("GS%d" % c), ind(w_win, v("NGU%d" % c, 64, 96)))
        gather_sub(c, 0)
        mm(v(k, 0, 287), one("ONB", 0, 128), one("CODE", 288 * e, 288 * e + 287), True, False)
        if e == 0:
            mm(v(k, 144, 287, 18), v("ELX", 256 * t + 128 * c, 256 * t + 128 * c + 128), v("ALF"), False, False)
        elif e < 4:
            mm(v(k, 0, 287, 18), v("IDF"), v("PU%d" % c, 17, 288, 18), False, False)
        absd(c, 0)
        mm(v("S%d" % c), v("XTN%d" % c), v("REP", 1024, 1536), True, False)
        mm(v("S%d" % c), v("IDB"), v("GS%d" % c), False, True)
        mm(v(k, 143, 287), ngf, v("ADF"), False, False)
        gather_sub(c, 1)
        if e == 0:
            tt(v("D0%d" % c), ind(w_win, ul), v("XI0", 256 * t + 128 * c, 256 * t + 128 * c + 128), A.subtract)
        absd(c, 1)
        absd(c, 2)
        if e == 0:
            act(v("A0%d" % c), v("D0%d" % c), F.Abs)
            mm(v(k, 0, 144, 18), v("A0%d" % c), v("BO"), False, False)

    def front2(c):
        dist(c, 0, 3)
        gather_sub(c, 2)
        absd(c, 3)
        dist(c, 3, 4)
        close("K%d" % c, 0, 287)

    def post1(e, c):
        k = "K%d" % c
        pu, x = ("PU%d" % c, v("EX%d" % c)) if e < 4 else ("PUV%d" % c, v("EXV%d" % c))
        p, u, nr = v(pu, 0, 144), v(pu, 144, 288), v("NR%d" % c)
        scan(p, v("RST"), v(k, 0, 144), BIG, A.max, A.min)
        tt(nr, p, v(k, 0, 144), A.is_lt)
        scan(u, v(k, 143, 287), nr, 0.0, A.add, A.mult)
        tt(x, ind(u, v("REPL")), v("MASK", 0, 128), A.mult)
        if e < 4:
            mm(v("L%d" % c, 0, 8), x, v("ALF"))
        else:
            mm(v("L%d" % c, 0, 24), x, v("ALN"), True, False)
            mm(v("L%d" % c, 0, 24), v("EX%d" % c), v("ALM"), False, True)

    def rows(c, pu, x):
        act(v("RU%d" % c), ind(v(pu, 144, 288), v("REPL")))
        mm(v("M%d" % c, x, 256, 2), v("RU%d" % c), v("IDF"))

    def post2(e, c):
        if e < 4:
            tc(v("LUV", 8 * c, 8 * c + 8), v("L%d" % c, 0, 8))
        else:
            tc(v("LUV", 16 + 8 * c, 24 + 8 * c), v("L%d" % c, 0, 8))
            rows(c, "PUV%d" % c, 1)
            act(v("NEGA", 8 * c, 8 * c + 8), v("L%d" % c, 8, 16))
            act(v("ABD", 8 * c, 8 * c + 8), v("L%d" % c, 16, 24), F.Abs)

    def winners(c):
        tt(v("FARB", 8 * c, 8 * c + 8), v("PU%d" % c, 17, 144, 18), v("TH128"), A.is_ge)
        rows(c, "PU%d" % c, 0)
        act(v("UVS", 16 + 8 * c, 24 + 8 * c), v("PU%d" % c, 161, 288, 18))

    def put(name, src):
        scat(v(name, 0, 3168), v("OUV"), v(src, 0, 512))

    def packed():
        ts(v("N0", 256, 512), v("N0", 256, 512), 131071, A.bitwise_and)
        put("PK", "N0")

    def merge(t):
        for j in range(3):
            tt(v("XM", j, 96, 3), v("RX%d_%d" % (t - 1, j), j, 96, 3), v("XE", 160 + j, 256, 3), A.max)
        ts(v("XM", 96, 192), v("XM", 0, 96), 255, A.bitwise_and)
        ts(v("XM", 192, 288), v("XM", 0, 96), 8, A.logical_shift_right, 4095, A.bitwise_and)
        tc(v("XI0", 256 * t + 160, 256 * t + 256), v("XM", 96, 192))
        el = v("ELX", 256 * t + 160, 256 * t + 256)
        tt(el, v("XM", 192, 288), v("MASK", 160, 256), A.mult)
        scan(v("OF", 0, 96), v("SEG"), el, 0.0, A.mult, A.add)
        tc(v("ELU", 16 * t + 10, 16 * t + 16), v("OF", 15, 96, 16))
        prep_t(t, 1)
        prep_s(1)
        prep_x(t, 1, (1, 2))
        if t < T_ - 1:
            prep_e(t, 160)

    def walks(t):
        prev = None
        for e in range(5):
            for c in range(2):
                front1(t, e, c)
                if prev:
                    post1(*prev)
                if t and e == 0 and c == 0:
                    merge(t)
                front2(c)
                if t and e == 0 and c == 0:
                    packed()
                if prev:
                    post2(*prev)
                if e == 4:
                    winners(c)
                prev = (e, c)
        post1(*prev)
        count(t, range(4), 0)
        post2(*prev)
        count(t, range(4, 8), 0)
        count(t, range(8), 1)
        count(t, range(8, 16), 1)

    nc = [0]

    def between(t, rc, a):
        if rc == 0 and a < 4 and t == 0:
            tc(v("PK", 600 * a, 600 * a + 600), v("NBI", 600 * a, 600 * a + 600))
        for c in range(2):
            if (rc, a) == (0, 4 + c):
                tc(v("EPU", 128 * c, 128 * c + 128), ind(pk_win, v("LUV", 8 * c, 8 * c + 8)))
            if (rc, a) == (1, c):
                tc(v("EP", 256 + 128 * c, 384 + 128 * c), ind(pk_win, v("LUV", 16 + 8 * c, 24 + 8 * c)))

    def count(t, blocks, rc):
        if blocks[0] == 0 and rc == 0:
            mm(v("K0", 480, 496), one("ONB", 0, 128), one("ZB", 0, 16), True, False)
        for a in blocks:
            own = a // 8 == rc
            lo = 64 * (a // 2 % 4) if own else 0
            ab, eq, r = v("AB%d" % (nc[0] % 3), 0, 256 - lo), "EQ%d" % (nc[0] % 4), lo // 2
            nc[0] += 1
            act(ab, v("M%d" % rc, lo, 256), F.Abs, bias=v("NEGA", a, a + 1), scale=2.0)
            ts(v(eq, 0, 256 - lo), ab, v("ABD", a, a + 1), A.is_equal)
            part = [(0, 128, "WX")]
            if own:
                part = [(r, 32, "WD%d" % (a % 2))]
                part += [(r2, n2, "WX") for r2, n2 in {0: ((32, 32), (64, 64)), 32: ((64, 64),), 64: ((96, 32),), 96: ()}[r]]
            for pr, pn, wt in part:
                s0 = 2 * pr - lo
                for x in range(2):
                    mm(v("K0", 480 + 8 * rc, 488 + 8 * rc, 1, pr + pn, pr), v(eq, s0 + x, s0 + 2 * pn, 2), v(wt), False, False)
            between(t, rc, a)
        if blocks[-1] == 15:
            close("K0", 480, 496)

    def lists(kind, lo):
        for c in range(2):
            j = 128 * (2 * kind + c)
            mm(v("L0", lo + 8 * c, lo + 8 * c + 8), v("EXZ", j, j + 128), v("ALB"))

    def send(t):
        tr, src, n = [], v("XC%d" % t, 0, 96), 4
        for j in range(3):
            dst = T.cores[(rank + 1 + j) % NB_]
            rid, pid = topo.addr(dst)[:2]
            eng = topo.engines(core, dst)
            n = 4 if len(eng) >= 12 else 2
            m = sum(1 << x for x in eng[n * j:n * j + n])
            key, b = "r%d_%d" % (t, j), "RX%d_%d" % (t, j)
            unit[key] = (T.sem["rx%d_%d" % (t, j)], n)
            hist[(key, 1)] = {}
            cnt[key] = 1
            acc[b] = [(key, 1, 0, 96, 0, 128, 1, True)]
            tr.append(RemoteDMATransfer(dst_ids=[DstId(rid=rid, pnc=pid)], dma_engine_mask=m, remote_sem=T.sem["rx%d_%d" % (t, j)], src=src[0], dst=T[b][:, 0:96]))
        unit["l%d" % t] = (T.sem["lx%d" % t], 3 * n)
        access("g", "l%d" % t, (), src[1])
        g.remote_dma_fused(tr, local_sem=T.sem["lx%d" % t])

    def edit(t):
        last, base = t == T_ - 1, L_ + 64 * t
        vl = v("LUV", 16, 32)
        xs = v("XI0", 256 * t, 256 * t + 256)
        wn, pn = v("W", base, base + 64), v("PK", base, base + 64)

        def mix(bank, lo, a, f1, f2, k):
            o = v(bank, lo, lo + 256)
            mm(o, v("MIX", 128 * f1, 128 * f1 + 128), v("WUV", a, a + 256), True, False)
            mm(o, v("MIX", 128 * f2, 128 * f2 + 128), xs, False, False)
            mm(o, v("CB", 128 * k, 128 * k + 128), v("ONB"), False, True)

        def slots():
            for b in range(4):
                k1, j = v("K1", 128 * b, 128 * b + 128), 128 * b
                mm(k1, two("CR2", 0, 128), two("ONB", 0, 128), True, False)
                mm(k1, v("BIGI", 0, 128), v("ZK", j, j + 128), False, False)
                mm(k1, v("KR", j, j + 128), v("BIGI", 128, 256), False, False)
                mm(k1, v("TGR", j, j + 128), v("IDF"), False, True)

        act(v("AGE", 0, 256), v("EPU"), F.Identity, bias=v("KC", 0, 1), scale=2.0 ** -20)
        act(v("NGF", 256, 512), ind(id_win, vl))
        act(v("AGE", 256, 512), v("EP", 256, 512), F.Identity, bias=v("KC", 0, 1), scale=2.0 ** -20)
        for c in range(2):
            act(v("UVS", 8 * c, 8 * c + 8), v("PUV%d" % c, 161, 288, 18))
        act(v("WUV"), ind(w_win, v("LUV")))
        ts(v("Z", 0, 16), v("K0", 480, 496), v("THC"), A.is_lt)
        for i in range(2):
            tt(v("W2", 16 * i, 16 * i + 16), v("Z", 0, 16), v("FARB"), A.mult)
        mm(v("L1", 0, 32), v("TRI"), v("W2"), True, False)
        mm(v("L1", 8, 16), v("ONB", 0, 128), v("W2", 0, 8), False, False)
        mm(v("L1", 24, 32), v("ONB", 0, 128), v("W2", 16, 24), False, False)
        close("L1", 0, 32)
        for c in range(2):
            for y in range(2):
                j = 256 * y + 128 * c
                tt(v("K1", j, j + 128), v("NGF", j, j + 128), v("M%d" % c, 1 - y, 256, 2), A.is_equal)
        tc(v("LF"), v("LUV"))
        tt(v("UMD"), v("LF"), v("DUM"), A.subtract)
        ts(v("SPA"), v("L1", 0, 32), 64.0, A.is_le)
        tt(v("SPL"), v("SPA"), v("W2"), A.mult)
        tc(v("PC"), v("L1", 0, 16))
        ts(v("NBV"), v("L1", 0, 32), float(base - 1), A.add)
        if not last:
            tt(v("RES"), v("FARB"), v("SPL", 0, 16), A.subtract)
            mm(v("L1", 64, 80), v("TRI"), v("RES"), True, False)
            mm(v("L1", 72, 80), v("ONB", 0, 128), v("RES", 0, 8), False, False)
            close("L1", 64, 80)
        tt(v("ZK"), v("K1"), v("AGE"), A.max)
        for b in range(4):
            k0 = v("K0", 96 * b, 96 * b + 96)
            mm(k0, v("ZK", 128 * b, 128 * b + 128), v("SEL"), True, False)
            mm(k0, two("ONB", 0, 128), two("RC2", 0, 96), False, True)
        tt(v("TG1"), v("NBV"), v("UVS", 0, 32), A.subtract)
        tt(v("TG2"), v("SPL"), v("TG1"), A.mult)
        tt(v("TG"), v("TG2"), v("UVS", 0, 32), A.add)
        if not last:
            ts(v("SN", 0, 16), v("L1", 64, 80), 96.0, A.is_le)
            tt(v("SN", 16, 32), v("SN", 0, 16), v("RES"), A.mult)
            tt(v("Z", 32, 48), v("SN", 16, 32), v("L1", 64, 80), A.mult)
            tt(v("EXZ", 256, 512), ind(v("Z", 32, 48), v("ZREP", 0, 16)), v("MASKB"), A.mult)
            lists(1, 48)
        tt(v("EXZ", 0, 256), ind(v("Z", 0, 16), v("ZREP", 0, 16)), v("MASKB"), A.mult)
        lists(0, 0)
        lists(0, 16)
        mix("S1", 0, 0, 0, 1, 0)
        mix("S1", 256, 256, 2, 3, 1)
        scan(v("KM"), v("RST12"), v("K0", 0, 384), BIG, A.max, A.min)
        act(v("TGR", 0, 256), ind(v("TG"), v("ZREP", 0, 16)))
        act(v("TGR", 256, 512), ind(v("TG"), v("ZREP", 16, 32)), F.Identity, bias=v("KC", 4, 5))
        act(v("T1"), v("EPU"), F.Relu, bias=v("KC", 3, 4), scale=-1.0)
        act(v("KR"), ind(v("KM"), v("K12R")))
        if not last:
            slots()
            z, o, o2 = v("L0", 48, 64), v("OF", 48, 64), v("OF", 112, 128)
            ts(o, z, 0.0, A.is_equal)
            tt(o2, o, v("DZR"), A.mult)
            tt(o, o2, z, A.add)
            ts(v("ORR"), o, -1.0, A.add)
            scat(v("XC%d" % t, 0, 352), v("ORR"), v("XE"), True)
            send(t)
        tt(v("OF", 128, 160), v("L0", 0, 32), v("UMD"), A.mult)
        tt(v("OF", 160, 192), v("OF", 128, 160), v("DUM"), A.add)
        tc(v("OUV"), v("OF", 160, 192))
        for c in range(2):
            for k in range(8):
                ts(v("C%d" % c, 64 * k, 64 * k + 64), v("KX"), v("PC", 8 * c + k, 8 * c + k + 1), A.is_ge)
        if not last:
            prep_t(t + 1, 0)
        for a in range(4):
            for c in range(2):
                mm(v("L0", 32 + a, 33 + a), v("C%d" % c, a, 512, 4), v("ONB", 0, 1), c == 0, c == 1)
        act(v("R1", 0, 512), v("S1"), F.Identity, bias=v("KC", 1, 2))
        act(v("WNB"), v("R1", 0, 512), F.Identity, bias=v("KC", 2, 3))
        put("W", "WNB")
        act(v("AQ"), v("T1"), F.Identity, bias=v("COLS", 2, 3), scale=-1.0)
        act(v("S1", 0, 256), v("T1"), F.Relu, bias=v("KC", 5, 6), scale=-65535.0)
        for c in range(2):
            act(v("NR2", 128 * c, 128 * c + 128), ind(v("UVS"), v("NLST", 8 * c, 8 * c + 8)))
        act(v("NA"), v("EPU"), F.Identity, bias=v("COLS", 4, 5), scale=v("COLS", 3, 4))
        if not last:
            prep_s(0)
            prep_x(t + 1, 0, (0, 1))
        mix("S0", 0, 0, 4, 4, 2)
        act(v("R1", 512, 768), v("S0", 0, 256), F.Identity, bias=v("KC", 1, 2))
        act(v("HX", 0, 256), v("R1", 512, 768), F.Identity, bias=v("KC", 2, 3))
        if last:
            slots()
        for c in range(2):
            mm(v("L1", 256 + 128 * c, 384 + 128 * c), v("NR2", 128 * c, 128 * c + 128), v("IDF"))
        if not last:
            prep_x(t + 1, 0, (2,))
            prep_t(t + 1, 1)
            prep_s(1)
            prep_e(t + 1, 0 if t + 1 < T_ - 1 else 160)
            prep_x(t + 1, 1, (0,))
        if last:
            tc(v("NL"), v("L0", 32, 36))
            tc(wn, ind(v("HX", 0, 257), v("NL")))
            for lo, hi, q in ((0, 1328, "y"), (1328, 2656, "s")):
                dma(q, T.yw[:, lo:hi], T.W[:, lo:hi], (), v("W", lo, hi)[1])
        tt(v("EP", 0, 256), v("AQ"), v("S1", 0, 256), A.max)
        tt(v("N0"), v("EP"), v("K1"), A.min)
        if not last:
            ts(v("NI"), v("N0"), 4095, A.bitwise_and)
            put("IDS", "NI")
            tc(v("NL"), v("L0", 32, 36))
            tc(wn, ind(v("HX", 0, 257), v("NL")))
        tt(v("NX", 0, 256), v("NA"), v("L1", 256, 512), A.add)
        tc(pn, ind(v("NX", 0, 257), v("NL")))
        if not last:
            tc(v("QI"), pn)
            ts(v("QI"), v("QI"), 4095, A.bitwise_and)
            tc(v("IDS", base, base + 64), v("QI"))
        else:
            packed()
            for lo, hi, q in ((0, 1328, "y"), (1328, 2656, "s")):
                dma(q, T.yn[:, lo:hi], T.PK[:, lo:hi], (), v("PK", lo, hi)[1])

    for t in range(T_):
        walks(t)
        edit(t)
    for src in sorted(cnt):
        wait("g", src, cnt[src])
